import numpy as np, ml_dtypes
CORES = [2,6,10,14,18,22,26,30]
N = 8
BF = ml_dtypes.bfloat16
def gentries(a):
    return np.ascontiguousarray(a.reshape(8, 16, -1).transpose(0, 2, 1)).reshape(8, -1)
def gtable(e):
    e = np.asarray(e); return np.ascontiguousarray(e.reshape(8, -1, 16).transpose(0, 2, 1)).reshape(128, -1).astype(np.int32)
W, WC, FR, X, H, V, FO = 4096, 4096, 3, 1536, 1, 8, 2
def loud(rng, lo, hi):
    v = 0.25 + 0.75 * rng.random((N, 8, 16, W), dtype=np.float32)
    return v * np.exp2(rng.integers(lo, hi + 1, (N, 8, 1, W)))
def perms(rng):
    return np.argsort(rng.random((N, 8, FR, W)), axis=-1)
def recs(rng):
    return 0.75 + 0.5 * rng.random((N, 8, 16, WC))
def turns(rng):
    return rng.integers(0, WC, (N, 8, W)), rng.integers(0, 4096, (N, 8, FR))
def put(a, m, v):
    i = int(np.argmax(a == v)); a[i] = a[m]; a[m] = v
def saw():
    n = np.arange(W)[None, :]; top = (16 - np.arange(16)[:, None]) % 16
    return 1.0 - np.where(n < top, top - n, (n - top) % 16) * 0.03125
def spikes(rng):
    v = 0.3125 + 0.5 * rng.random((N, 8, 16, W))
    n = rng.choice(np.array([0, 1, V - 1, V - 1, V, V, V + 1, 15, 16]), (N, 8, 1, W // 8))
    a = np.argsort(rng.random((N, 8, 16, W // 8)), axis=2) < n; k = rng.integers(0, 4, a.shape); miss = ~a & (k == 3)
    v[..., ::8] = np.where(a | miss, 1.0, 0.25)
    v[..., H::8] = np.where(miss, 1.0078125, np.where(a & (k == 1), 1.0, v[..., H::8]))
    v[..., H + 1::8] = np.where(a & (k == 2), 1.0078125, v[..., H + 1::8])
    return v
RATES = np.concatenate([np.arange(192, 256), np.arange(256, 321, 2)])
def near(k):
    s = np.concatenate([np.arange(128, 256), np.arange(256, 512, 2), np.arange(512, 1024, 4)]).astype(np.int64)
    a = np.tile(np.arange(RATES.size), s.size); s = np.repeat(s, RATES.size)
    x = s * RATES[a].astype(np.int64) ** k; b = x.astype(np.float32).view(np.int32)
    o = np.argsort(x, kind="stable"); i, j = o[:-1], o[1:]
    low = (b[i] != b[j]) & ((b[i] >> 2) == (b[j] >> 2)); tie = (x[i] != x[j]) & (b[i] == b[j])
    return s, a, [np.stack([i[w], j[w]], axis=1) for w in (low, tie) if np.any(w)]
def plant(rng, found, S, C, P, R, q, g):
    s, a, L = found; h = (W - (FR - 1) * X) // 8; n = 8 * np.arange(h)
    v = (1.0 + 0.5 * rng.random((16, 8 * h))) * 0.0625
    e = np.stack([L[int(w)][int(rng.integers(0, len(L[int(w)])))] for w in rng.integers(0, len(L), h)])
    e = np.where(rng.random((h, 1)) < 0.5, e, e[:, ::-1])
    on = np.argsort(rng.random((16, h)), axis=0) < rng.choice(np.array([V, V, 16]), h)
    for i in range(2):
        v[:, n + 3 + i] = np.where(on, s[e[:, i]] * 2.0 ** -8, v[:, n + 3 + i]); R[q, g, n + 3 + i] = a[e[:, i]]
    S[q, g, :, :8 * h] = v; C[q, g, :, :RATES.size] = RATES * 0.00390625; P[q, g, :FR - 1] = np.arange(W)
def pack(S, C, P, R, hp):
    return {"sp": np.ascontiguousarray(S.reshape(N, 128, W)).astype(BF), "rec": np.ascontiguousarray(C.reshape(N, 128, WC)).astype(BF), "itg": np.stack([gtable(a.reshape(8, FR * W)) for a in P]),
            "rot": np.ascontiguousarray(R).astype(np.int32), "hop": np.ascontiguousarray(hp).astype(np.int32)}
def setup_inputs(rng):
    S = loud(rng, -1, 1); C = recs(rng); P = perms(rng); R, hp = turns(rng)
    return pack(S, C, P, R, hp)
def setup_inputs_spread(rng):
    S = loud(rng, 0, 0) * rng.choice(np.array([0.5, 2.0]), (N, 8, 1, W)); C = recs(rng); P = perms(rng)
    R = np.exp2(np.log2(WC) * rng.random((N, 8, W))).astype(np.int64) - 1; R = np.where(rng.random(R.shape) < 0.5, R, WC - 1 - R)
    hp = np.exp2(12 * rng.random((N, 8, FR))).astype(np.int64) - 1
    found = near(FR - 1)
    for q in range(N):
        for g in range(8):
            if (q + g) % 4 == 1: plant(rng, found, S, C, P, R, q, g)
    return pack(S, C, P, np.clip(R, 0, WC - 1), np.clip(hp, 0, 4095))
def setup_inputs_ends(rng):
    share = rng.choice(np.array([0.0, 0.75, 1.0, 1.0]), (N, 8, 1, W)); share[..., 0] = 1.0; share[..., W - 1] = 1.0
    S = np.where(rng.random((N, 8, 16, W)) < share, 4.0, 0.0625)
    C = np.where(rng.random((N, 8, 16, WC)) < 0.5, 0.75, 1.25); C[..., 0] = 0.75; C[..., WC - 1] = 1.25
    P = perms(rng); R = rng.integers(0, 2, (N, 8, W)) * (WC - 1); hp = rng.integers(0, 2, (N, 8, FR)) * 4095
    hp[:, 1, 0] = 0; hp[:, 2, 0] = 4095
    for q in range(N):
        for g in range(8):
            k = (q + g) % 4
            if (q, g) in ((0, 0), (N - 1, 7)): k = 0; hp[q, g, 0] = 4095; R[q, g, 0] = WC - 1; R[q, g, W - 1] = 0
            if k == 0: P[q, g] = np.arange(W)[::-1]
            elif k == 2: P[q, g, ::2] = np.arange(W)
            else:
                for t in range(FR): put(P[q, g, t], 0, W - 1); put(P[q, g, t], W - 1, 0)
    return pack(S, C, P, R, hp)
def setup_inputs_corners(rng):
    S = loud(rng, -1, 1); C = recs(rng); P = perms(rng); R, hp = turns(rng); sk = spikes(rng); teeth = saw()
    for q in range(N):
        for g in range(8):
            k = (q + g) % 8
            if k == 0: S[q, g] = 0.75
            elif k == 1:
                S[q, g] = teeth; C[q, g] = 1.0
                for t in range(FR): put(P[q, g, t], (W - 1, 0, W // 2, W - 1)[q % 4], 0)
            elif k == 2: S[q, g] = sk[q, g]; P[q, g] = np.arange(W)
            elif k == 3: S[q, g] = sk[q, g]; P[q, g] = np.arange(W)[::-1]
            elif k == 4: S[q, g] = np.where(np.repeat(rng.random(W // 64) < 0.6, 64), S[q, g], 0.0625)
            elif k == 5: P[q, g] = (np.arange(W) + 1) % W
            elif k == 6:
                v = teeth.copy(); v[:, W - 1] = 1.5; S[q, g] = v
                for t in range(FR): put(P[q, g, t], 100, W - 1); put(P[q, g, t], 300, 0)
            else: R[q, g] = rng.integers(0, 2, W) * (WC - 1); hp[q, g] = rng.integers(0, 2, FR) * 4095
    for q, place in ((1, 0), (3, W - 1)):
        for a, g in ((q - 1, 5), (q - 1, 6), (q - 1, 7), (q, 7)):
            S[a, g] = teeth; P[a, g] = perms(rng)[a, g]; P[a, g, :FR - 1] = np.arange(W); R[a, g] = rng.integers(0, 4, W)
            C[a, g] = 0.75 + 0.5 * rng.random((16, WC)); C[a, g, :, :4] = 1.0
        put(P[q, 7, FR - 1], place, 0); hp[q, 7, FR - 1] = 4095
    return pack(S, C, P, R, hp)
def setup_inputs_crowd(rng):
    S = np.zeros((N, 8, 16, W)); C = recs(rng); P = perms(rng); R, hp = turns(rng); teeth = saw(); flat = (16, 15, V + 1, V, V - 1, V - 2, 1, 0)
    for q in range(N):
        for g in range(8):
            v = teeth.copy(); v[rng.permutation(16)[:flat[(q + g) % 8]]] = 0.75; S[q, g] = v * 0.125
    C[::2] = 0.75 + 0.0078125 * rng.integers(0, 65, C[::2].shape[:3] + (1,))
    return pack(S, C, P, R, hp)
def setup_inputs_calm(rng):
    S = spikes(rng) * 0.25; C = recs(rng); C[::2] = 1.0; R, hp = turns(rng); hp[:] = 0
    few = rng.choice(np.array([0, 1, 2, 3, 8, W - 1, W - 8]), (N, 8, FR, 1)); P = (np.arange(W) + few) % W
    R = np.where(np.arange(8)[None, :, None] % 2 == 0, rng.integers(0, 4, R.shape), rng.integers(WC - 2, WC, R.shape))
    C[1::2, :, :, [0, 1, 2, 3, WC - 2, WC - 1]] = np.array([0.75, 0.875, 1.0, 1.125, 1.25, 0.8125])
    return pack(S, C, P, R, hp)
def check_ranges(d):
    bad = []
    for k, lo, hi in (("itg", 0, W - 1), ("rot", 0, WC - 1), ("hop", 0, 4095)):
        if np.min(d[k]) < lo or np.max(d[k]) > hi: bad.append("range of " + k)
    p = np.sort(np.stack([gentries(a) for a in d["itg"]]).reshape(N, 8, FR, W), axis=-1)
    if not np.all(p == np.arange(W)): bad.append("itg: no permutation")
    s = np.asarray(d["sp"]).astype(np.float64); c = np.asarray(d["rec"]).astype(np.float64)
    if not np.all((s >= 0.0625) & (s <= 4)): bad.append("range of sp")
    if not np.all((c >= 0.75) & (c <= 1.25)): bad.append("range of rec")
    return bad
def reference(sp, rec, itg, rot, hop):
    S = sp.astype(np.float32).reshape(N, 8, 16, W); C = rec.astype(np.float32).reshape(N, 8, 16, WC); R = rot.astype(np.int64); hp = hop.astype(np.int64)
    P = np.stack([gentries(a) for a in itg]).astype(np.int64).reshape(N, 8, FR, W); m = np.arange(W)
    for t in range(FR):
        vote = np.ones(S.shape, bool)
        for d in range(1, H + 1):
            vote[..., d:] &= S[..., d:] >= S[..., :-d]; vote[..., :-d] &= S[..., :-d] >= S[..., d:]
        peak = np.add.reduce(vote, axis=2, dtype=np.int64) >= V; peak[..., 0] = True
        it = P[:, :, t]; moved = np.take_along_axis(peak, it, 2)
        left = np.maximum.accumulate(np.where(moved, m, -2 * W), axis=-1)
        right = np.minimum.accumulate(np.where(moved, m, 3 * W)[..., ::-1], axis=-1)[..., ::-1]
        q = np.where(m - left <= right - m, left, right); p = np.take_along_axis(it, q, 2)
        src = np.clip(p + m - q, 0, W - 1)
        T = np.take_along_axis(S, src[:, :, None, :], 3)
        Q = (np.take_along_axis(R, src, 2) + hp[:, :, t, None] * (q - p)) & (WC - 1)
        T = np.concatenate([np.roll(T[..., W - X:], (1, t), axis=(0, 1)), T[..., :W - X]], axis=-1)
        R = np.concatenate([np.roll(Q[..., W - X:], (1, t), axis=(0, 1)), Q[..., :W - X]], axis=-1)
        S = T * np.take_along_axis(C, R[:, :, None, :], 3)
    y = np.add.reduce(S.astype(np.float64).reshape(N, 128, FO, W // FO), axis=2)
    return {"y": y.astype(np.float32)}

def check_inputs(d):
    bad = list(check_ranges(d))
    if not bad:
        for name, y in reference(**d).items():
            for q in range(N):
                v = np.abs(np.asarray(y[q], np.float64)); s = np.sqrt(np.mean(v * v))
                if v.max() > 7 * s or s < 2.0 ** -3: bad.append('%s of rank %d is uneven or too small' % (name, q))
    return bad

@@ -1,0 +1,748 @@
+import numpy as np
+from concourse.bass import DstId, RemoteDMATransfer
+from concourse.mybir import AluOpType as ALU, AxisListType as AX, ActivationFunctionType as AF
+
+W, X, LOC = 4096, 1536, 2560
+F32, BF, I32, U16 = "float32", "bfloat16", "int32", "uint16"
+SCRATCH = {
+    "spa": ("sbuf", [128, W], BF), "spb": ("sbuf", [128, W + 16], BF),
+    "reca": ("sbuf", [128, W], BF), "recb": ("sbuf", [128, W], BF),
+    "Sx": ("sbuf", [128, W + 8], F32), "Sy": ("sbuf", [128, W + 8], F32),
+    "Tl": ("sbuf", [128, LOC], F32), "Ts": ("sbuf", [128, X], F32), "Ts0": ("sbuf", [128, X], BF),
+    "L0": ("sbuf", [128, X], BF), "L1": ("sbuf", [128, X], F32), "L2": ("sbuf", [128, X], F32),
+    "V": ("sbuf", [128, W], BF), "Vg": ("sbuf", [128, W], BF), "Rw": ("sbuf", [128, W], BF),
+    "r2": ("sbuf", [128, W], BF), "mS": ("sbuf", [128, 256], F32), "r1": ("sbuf", [128, W], BF), "A": ("sbuf", [128, 2048], F32),
+    "Yo": ("sbuf", [128, 2048], F32),
+    "Q0": ("sbuf", [128, 256], U16), "Q1": ("sbuf", [128, 256], U16), "Q2": ("sbuf", [128, 256], U16),
+    "Qs": ("sbuf", [128, 288], U16), "Qi": ("sbuf", [128, 256], I32), "Qx": ("sbuf", [128, 256], I32),
+    "Qf": ("sbuf", [128, 256], F32), "HL": ("sbuf", [128, 512], BF),
+    "it": ("sbuf", [128, 768], I32), "it16": ("sbuf", [128, 768], U16), "itT": ("sbuf", [128, 8, 96], I32),
+    "E": ("sbuf", [128, 768], F32), "En": ("sbuf", [128, 768], F32),
+    "cI": ("sbuf", [128, 8, 32], F32), "Xc": ("sbuf", [128, 256], F32), "Z2": ("sbuf", [128, 160], BF),
+    "Wn": ("sbuf", [128, 512], F32), "W1": ("sbuf", [128, 16, 32], F32),
+    "C1": ("sbuf", [128, 64], F32), "C2": ("sbuf", [128, 64], F32), "C3": ("sbuf", [128, 64], F32),
+    "tt": ("sbuf", [128, 256], F32), "ch": ("sbuf", [128, 256], I32), "ee": ("sbuf", [128, 256], I32),
+    "en": ("sbuf", [128, 256], I32), "su": ("sbuf", [128, 256], F32), "hd": ("sbuf", [128, 256], F32),
+    "s16": ("sbuf", [128, 256], U16), "s16a": ("sbuf", [128, 160], U16),
+    "rs": ("sbuf", [128, 256], I32), "hrow": ("sbuf", [128, 32], I32), "hb": ("sbuf", [128, 32], I32),
+    "hm": ("sbuf", [128, 24], F32), "nh": ("sbuf", [128, 4], F32),
+    "i1": ("sbuf", [128, 160], I32), "i2": ("sbuf", [128, 160], I32), "i3": ("sbuf", [128, 160], I32),
+    "pc": ("sbuf", [128, 4], I32), "pm": ("sbuf", [128, 4], I32), "pf": ("sbuf", [128, 4], F32),
+    "kb": ("sbuf", [128, 32], BF), "mk": ("sbuf", [128, 256], F32),
+    "Iw": ("sbuf", [128, 160], F32), "In": ("sbuf", [128, 128], F32), "Ib": ("sbuf", [128, 128], BF),
+    "Inb": ("sbuf", [128, 128], BF), "Z": ("sbuf", [128, 160], BF), "Ym": ("sbuf", [128, 2304], BF),
+    "pv": ("psum", [128, 2048], F32), "pa": ("psum", [128, 512], F32), "pb": ("psum", [128, 512], F32),
+    "pk": ("psum", [128, 512], F32), "pt": ("psum", [128, 512], F32),
+}
+NDMA = 48
+SEMAPHORES = ["v", "a", "t", "p", "sent"] + ["d%d" % i for i in range(NDMA)] + ["s%d" % i for i in range(12)] + \
+    ["r%d" % i for i in range(12)] + ["h%d" % i for i in range(6)]
+ROWED = ("spa", "spb", "reca", "recb", "it", "rs", "Rw", "hrow", "cI", "y")
+BIG = float(2 ** 26)
+P5 = [0, 32, 64, 96, 128, 160]
+SPAN = {}
+LOC01 = [("R", "v", 0, 32), ("T", "a", 0, 32), ("R", "a", 32, 96), ("R", "a", 96, 160), ("T", "a", 32, 64),
+         ("T", "a", 64, 96), ("T", "a", 96, 128), ("T", "a", 128, 160)]
+LOC2 = [("R", "a", 0, 64), ("R", "a", 64, 128), ("T", "a", 0, 32), ("R", "a", 128, 160), ("T", "a", 32, 64),
+        ("T", "a", 64, 96), ("T", "a", 96, 128), ("T", "a", 128, 160)]
+OPT = {"hd": "a", "pj": 0, "tslack": 0.0, "tries": 1, "noise": 1.0, "relay": True, "halves": 2, "strict": False,
+       "pe": 0.45e-3, "gat": 1.56, "dbw": 400e3, "wake": 0.08, "slack": 0.0,
+       "rlat": (4.0, 6.0, 8.0, 5.0), "m0": "qpqpqpqppp",
+       "sp": [0, 1024, 2560, 4096],
+       "c0": [1, 512, 1023, 1534, 2045, 2556, 3067, 3578, 3840, 4096], "rc": [1, 511, 1022, 1280, 1537],
+       "lc": [1537, 2047, 2558, 3069, 3580, 3840, 4096], "lag": 512,
+       "lmode": "zazaza", "rmode": "zaaa", "ve": ["avavavav"] * 3, "te": ["ava"] * 3,
+       "rt": [[("v", 160, 256)]] * 3,
+       "loc": [LOC01, LOC01, LOC2]}
+
+
+def route(T, topo, rank):
+    src = T.cores[rank]
+    dst = T.cores[(rank + 1) % len(T.cores)]
+    eng = topo.engines(src, dst)
+    relay = None
+    if topo.chip(src) != topo.chip(dst) and OPT["relay"]:
+        for c in topo.cores_of(src):
+            if T.rank_of(c) is None and topo.die(c) != topo.die(src) and topo.may_write(c, dst):
+                relay = c
+    if relay is not None:
+        first = [e for e in topo.engines(src, relay) if e not in eng]
+        second = eng
+    else:
+        first, second = eng[len(eng) // 2:], eng[:len(eng) // 2]
+    whole = second if relay is not None or topo.chip(src) == topo.chip(dst) else eng
+    return dst, [(1024, X, relay, first), (0, 512, None, second), (512, 1024, None, whole)], whole
+
+
+def bits(engines):
+    return sum(1 << e for e in engines)
+
+
+def relay_program(g, core, T, topo):
+    for rank in range(len(T.cores)):
+        dst, pieces, _e = route(T, topo, rank)
+        for i, (a, b, relay, eng) in enumerate(pieces):
+            if relay != core:
+                continue
+            rid, pid, _s = topo.addr(dst)
+            on = topo.engines(core, dst)
+            for t in range(3):
+                buf = T["L%d" % t]
+                g.wait_ge(T.sem["h%d" % t], len(eng))
+                g.remote_dma(buf[:, a:b], buf[:, a:b], T.sem["r%d" % (4 * t + i)], T.sem["sent"], pid, rid, bits(on))
+            g.wait_ge(T.sem["sent"], 3 * len(on))
+
+
+def rank_program(g, core, T, topo):
+    rank = T.rank_of(core)
+    if rank is None:
+        relay_program(g, core, T, topo)
+        return
+    N = len(T.cores)
+    Q = {"v": g.vector, "a": g.scalar, "t": g.tensor, "p": g, "s": g.sync}
+    ops = []
+    shapes = {k: v[1] for k, v in SCRATCH.items()}
+    shapes["y"] = [128, 2048]
+    grid = {}
+    last_w = {}
+    readers = {}
+
+    def R(name, *idx):
+        idx = idx if idx else (slice(None),)
+        return (name, idx, T[name][idx if len(idx) > 1 else idx[0]])
+
+    def G(win, off):
+        return (win, off, win[2].indirect(off[2]))
+
+    def cells(ref):
+        name, idx = ref[0], ref[1]
+        sh = shapes[name]
+        if name not in grid:
+            n = int(np.prod(sh[1:]))
+            rows = 128 if name in ROWED else 1
+            grid[name] = np.arange(rows * n).reshape([rows] + list(sh[1:]))
+            last_w[name] = np.full(rows * n, -1, np.int32)
+            readers[name] = []
+        if name in ROWED:
+            c = grid[name][idx].ravel()
+        else:
+            c = grid[name][(slice(None),) + tuple(idx[1:])].ravel()
+        if SCRATCH.get(name, ("", ))[0] == "psum":
+            b = np.unique(c // 512)
+            c = (b[:, None] * 512 + np.arange(512)[None, :]).ravel()
+        return name, c
+
+    def flat(refs):
+        out = []
+        for r in refs:
+            if isinstance(r, tuple) and len(r) == 3:
+                if isinstance(r[0], tuple):
+                    out += [r[0], r[1]]
+                else:
+                    out.append(r)
+        return out
+
+    def width(ref):
+        if isinstance(ref[0], tuple):
+            return 16 * width(ref[1])
+        return int(np.prod(ref[2].shape[1:]))
+
+    def price(q, writes, reads):
+        full = [r for r in reads if isinstance(r, tuple)]
+        if q == "t":
+            return max(64, width(writes[0])) * OPT["pe"] * (4 if SCRATCH[full[0][0]][2] == F32 else 1)
+        n = width(writes[0])
+        if any(isinstance(r[0], tuple) for r in full):
+            return 0.055 + n * OPT["gat"] * 0.83e-3
+        if q == "p":
+            return 0.15 + n * 1.66e-3
+        big = [r for r in full if width(r) == n]
+        if len(big) == 2 and all(SCRATCH[r[0]][0] == "sbuf" for r in big) and n > 1:
+            n *= 2
+        return 0.03 + max(64, n) * 0.83e-3
+
+    def op(q, fn, writes, reads, sem=None, inc=1, cost=None, lat=0.0, after=()):
+        me = len(ops)
+        deps = set()
+        order = set(after)
+        for r in flat(reads):
+            if r[0] not in shapes:
+                continue
+            name, c = cells(r)
+            psum = SCRATCH.get(name, ("", ))[0] == "psum"
+            for d in np.unique(last_w[name][c]):
+                if d >= 0:
+                    deps.add(int(d))
+            if psum:
+                for (d, cc) in readers[name]:
+                    if ops[d]["q"] != q and np.any(cc[c]):
+                        deps.add(d)
+            m = np.zeros(last_w[name].size, bool)
+            m[c] = True
+            readers[name].append((me, m))
+        for r in flat(writes):
+            name, c = cells(r)
+            psum = SCRATCH.get(name, ("", ))[0] == "psum"
+            for d in np.unique(last_w[name][c]):
+                if d >= 0:
+                    same = ops[d]["q"] == q and sem is None and ops[d]["sem"] is None
+                    (order if same and q == "t" else deps).add(int(d))
+            keep = []
+            for (d, cc) in readers[name]:
+                if d != me and np.any(cc[c]):
+                    deps.add(d)
+                    cc[c] = False
+                if np.any(cc):
+                    keep.append((d, cc))
+            readers[name] = keep
+            last_w[name][c] = me
+        deps.discard(me)
+        if cost is None:
+            cost = price(q, writes, reads)
+        if q in "spr":
+            k = "p" if q == "r" else q
+            if k in chain:
+                (deps if q == "p" else order).add(chain[k])
+            chain[k] = me
+        ops.append({"q": q, "fn": fn, "deps": deps, "order": order, "sem": sem, "inc": inc, "cost": cost, "lat": lat})
+        return me
+
+    nd = [0]
+    chain = {}
+    moved_us = [0.0]
+
+    def dma(q, out, in_, load=True):
+        s = "d%d" % nd[0]
+        nd[0] += 1
+        us = int(np.prod(out[2].shape)) * (2 if SCRATCH.get(out[0], (0, 0, F32))[2] == BF else 4) / OPT["dbw"]
+        if load:
+            moved_us[0] += us
+            us = moved_us[0]
+        op(q, lambda: Q[q].dma_start(out[2], in_[2]), [out], [in_], sem=s, inc=16, cost=0.1, lat=2.0 + us)
+
+    def ap(x):
+        return x[2] if isinstance(x, tuple) else x
+
+    def tt(out, a, b, o):
+        op("v", lambda: g.vector.tensor_tensor(out[2], a[2], b[2], o), [out], [a, b])
+
+    def ts(out, a, s1, s2, o0, o1=None):
+        if o1 is None:
+            op("v", lambda: g.vector.tensor_scalar(out[2], a[2], ap(s1), None, o0), [out], [a, s1])
+        else:
+            op("v", lambda: g.vector.tensor_scalar(out[2], a[2], ap(s1), ap(s2), o0, o1), [out], [a, s1, s2])
+
+    def cp(out, a):
+        op("v", lambda: g.vector.tensor_copy(out[2], a[2]), [out], [a])
+
+    def tr(out, a):
+        op("v", lambda: g.vector.transpose(out[2], a[2]), [out], [a])
+
+    def scan(out, d0, d1, init, o0, o1):
+        op("v", lambda: g.vector.tensor_tensor_scan(out[2], d0[2], d1[2], init, o0, o1), [out], [d0, d1],
+           cost=0.03 + max(64, width(out)) * 0.83e-3)
+
+    def fill(out, c):
+        op("v", lambda: g.vector.memset(out[2], c), [out], [])
+
+    def act(out, a, f=AF.Copy, bias=0.0, scale=1.0):
+        if f == AF.Copy:
+            op("a", lambda: g.scalar.activation(out[2], a[2], f, scale=scale), [out], [a])
+        else:
+            op("a", lambda: g.scalar.activation(out[2], a[2], f, bias=bias, scale=scale), [out], [a])
+
+    def mm(out, l, r, start, stop):
+        op("t", lambda: g.tensor.matmul(out[2], l[2], r[2], start, stop), [out], [l, r])
+
+    def iota(out, pat, base, cm, small=False):
+        if small:
+            op("p", lambda: g.iota(out[2], pat, base, cm, allow_small_or_imprecise_dtypes=True), [out], [])
+        else:
+            op("p", lambda: g.iota(out[2], pat, base, cm), [out], [])
+
+    S = slice
+    ALL = S(None)
+
+    def turned(q2, buf, cols, src, scols, k, unit=16):
+        k %= 8
+        dma(q2[0], R(buf, S(0, 128 - 16 * k), cols), (src, None, T[src][unit * k:unit * 8, scols]))
+        if k:
+            dma(q2[1], R(buf, S(128 - 16 * k, 128), cols), (src, None, T[src][0:unit * k, scols]))
+
+    sp = OPT["sp"]
+    turned("ss", "spb", S(sp[0], sp[1]), "sp", S(sp[0], sp[1]), rank + 1)
+    turned("aa", "it", S(0, 256), "itg", S(0, 256), rank + 1)
+    turned("aa", "it", S(256, 768), "itg", S(256, 768), rank)
+    for i in range(1, len(sp) - 1):
+        turned("ss", "spb", S(sp[i], sp[i + 1]), "sp", S(sp[i], sp[i + 1]), rank + 1)
+    turned("ss", "rs", ALL, "rot", ALL, rank + 1, unit=1)
+    dma("s", R("hrow", S(0, 1), S(0, 3 * (8 - rank))), ("hop", None, T.hop[rank:8, :]))
+    dma("s", R("hrow", S(0, 1), S(3 * (8 - rank), 27)), ("hop", None, T.hop[0:rank + 1, :]))
+    turned("ss", "spa", ALL, "sp", ALL, rank)
+    turned("ss", "reca", ALL, "rec", ALL, rank)
+
+    iota(R("i1"), [[1, 160]], 112, -1)
+    iota(R("pc"), [[0, 4]], 0, 1)
+    fill(R("spb", ALL, S(W, W + 16)), 0.0)
+    ts(R("i2"), R("i1"), 127, None, ALU.bitwise_and)
+    ts(R("pm"), R("pc"), 15, None, ALU.bitwise_and)
+    ts(R("Ib"), R("i2", ALL, S(16, 144)), 0.0, None, ALU.is_equal)
+    ts(R("Inb"), R("i2", ALL, S(16, 144)), 0.0, -1.0, ALU.is_equal, ALU.mult)
+    cp(R("pf"), R("pm"))
+    ts(R("Iw"), R("i2"), 0.0, None, ALU.is_equal)
+    ts(R("In"), R("i2", ALL, S(16, 144)), 0.0, -1.0, ALU.is_equal, ALU.mult)
+    ts(R("i3"), R("i1"), R("pf", ALL, S(0, 1)), 112.0, ALU.add, ALU.add)
+    fill(R("V", ALL, S(0, 1)), 1.0)
+    ts(R("i3"), R("i3"), 127, None, ALU.bitwise_and)
+    fill(R("C2"), -BIG)
+    ts(R("Z"), R("i3"), 0.0, None, ALU.is_equal)
+    ts(R("pm", ALL, S(1, 2)), R("pc", ALL, S(1, 2)), 31, None, ALU.bitwise_and)
+    ts(R("pm", ALL, S(2, 3)), R("pc", ALL, S(2, 3)), 4, 1, ALU.logical_shift_right, ALU.bitwise_and)
+    tt(R("pf", ALL, S(1, 2)), R("pm", ALL, S(1, 2)), R("pm", ALL, S(2, 3)), ALU.subtract)
+    ts(R("Z2"), R("i1"), R("pf", ALL, S(1, 2)), 144.0, ALU.add, ALU.is_equal)
+    ts(R("Z2"), R("Z2"), 2 * BIG, None, ALU.mult)
+    fill(R("kb"), 2 * BIG)
+    fill(R("Sx", ALL, S(W, W + 8)), 0.0)
+    fill(R("Sy", ALL, S(W, W + 8)), 0.0)
+    iota(R("cI"), [[16, 8], [0, 2], [1, 16]], -2048, 128, True)
+    iota(R("mk"), [[16, 256]], -4096, 0, True)
+    iota(R("Rw"), [[0, W]], 0, 0, True)
+    op("p", lambda: g.partition_broadcast(T.hb[:, 0:27], T.hrow[0:1, 0:27], 128), [R("hb")], [R("hrow", S(0, 1), S(0, 27))])
+    iota(R("Ym"), [[0, 2304]], 1, 0, True)
+    op("p", lambda: g.affine_select(T.Ym[:], T.Ym[:], [[-1, 16], [-16, 9], [1000, 16]], ALU.is_equal, 0.0, -1000, 1),
+       [R("Ym")], [R("Ym")])
+    ts(R("pm", ALL, S(3, 4)), R("pc", ALL, S(3, 4)), 5, None, ALU.logical_shift_right)
+    ts(R("pf", ALL, S(2, 3)), R("pm", ALL, S(3, 4)), -4096.0, None, ALU.mult)
+    ts(R("cI"), R("cI"), R("pf", ALL, S(2, 3)), 8191.0, ALU.add, ALU.mult)
+    ts(R("cI"), R("cI"), 2048.0, None, ALU.add)
+
+    def late():
+        ts(R("pk", ALL, S(0, 256)), R("cI"), 2.0, None, ALU.mult)
+        ts(R("pk", ALL, S(256, 512)), R("mk"), R("pf", ALL, S(0, 1)), None, ALU.add)
+        if OPT["hd"] != "v":
+            ts(R("mS"), R("mk"), R("pf", ALL, S(0, 1)), 4096.0, ALU.add, ALU.add)
+
+    def lists(t0, t1):
+        for B in range(8):
+            cp(R("it16", ALL, S(96 * B + 32 * t0, 96 * B + 32 * t1)), R("it", ALL, S(256 * t0 + B, 256 * t1, 8)))
+
+    def keys_a(t0, t1):
+        for B in range(8):
+            tr(R("itT", ALL, B, S(32 * t0, 32 * t1)), R("it", ALL, S(256 * t0 + B, 256 * t1, 8)))
+
+    def keys(t):
+        for v in range(2):
+            tt(R("E", ALL, S(256 * t + v, 256 * t + 256, 2)), R("itT", ALL, ALL, S(32 * t + 16 * v, 32 * t + 16 * v + 16)),
+               R("cI", ALL, ALL, S(16 * v, 16 * v + 16)), ALU.add)
+        c = S(256 * t, 256 * t + 256)
+        act(R("En", ALL, c), R("E", ALL, c), scale=-1.0)
+
+    def hops():
+        for t in range(3):
+            o = 3 if t == 0 else t
+            tt(R("hm", ALL, S(8 * t, 8 * t + 8)), R("hb", ALL, S(o, o + 22, 3)), R("Z", ALL, S(32, 145, 16)), ALU.mult)
+        for t in range(3):
+            op("v", lambda t=t: g.vector.tensor_reduce(T.nh[:, t:t + 1], T.hm[:, 8 * t:8 * t + 8], AX.X, ALU.add, negate=True),
+               [R("nh", ALL, S(t, t + 1))], [R("hm", ALL, S(8 * t, 8 * t + 8))])
+
+    def first_rows():
+        cp(R("HL", ALL, S(0, 256)), R("rs"))
+        tt(R("HL", ALL, S(256, 512)), R("rs"), R("HL", ALL, S(0, 256)), ALU.subtract)
+        dma("s", R("Rw", S(0, 128, 16), ALL), R("HL", ALL, S(0, 256)), False)
+        dma("s", R("Rw", S(1, 128, 16), ALL), R("HL", ALL, S(256, 512)), False)
+
+    slot = [0]
+
+    def votes(Sn, a, b, mode):
+        w = b - a
+        if w > 511:
+            votes(Sn, a, a + w // 2, mode)
+            votes(Sn, a + w // 2, b, mode)
+            return
+        p0 = 512 * (slot[0] % 4)
+        slot[0] += 1
+        if mode in "pqz":
+            pos, neg = (R("Ib"), R("Inb")) if Sn == "spb" else (R("Iw", ALL, S(16, 144)), R("In"))
+            o = R("pv", ALL, S(p0, p0 + w + 1))
+            mm(o, pos, R(Sn, ALL, S(a - 1, b)), True, False)
+            mm(o, neg, R(Sn, ALL, S(a, b + 1)), False, True)
+            act(R("r1", ALL, S(a, b)), R("pv", ALL, S(p0, p0 + w)), AF.Relu, scale=float(2 ** 36))
+            nxt = R("pv", ALL, S(p0 + 1, p0 + w + 1))
+            if mode == "p":
+                tt(R("V", ALL, S(a, b)), nxt, R("r1", ALL, S(a, b)), ALU.subtract)
+            elif mode == "z":
+                act(R("r2", ALL, S(a, b)), nxt, AF.Relu, scale=-float(2 ** 36))
+                p1 = 512 * (slot[0] % 4)
+                slot[0] += 1
+                nxt = R("pv", ALL, S(p1, p1 + w))
+                mm(nxt, R("Inb"), R("r1", ALL, S(a, b)), True, False)
+                mm(nxt, R("Inb"), R("r2", ALL, S(a, b)), False, True)
+                act(R("V", ALL, S(a, b)), nxt)
+            else:
+                p1 = 512 * (slot[0] % 4)
+                slot[0] += 1
+                nxt = R("pv", ALL, S(p1, p1 + w))
+                mm(nxt, pos, R(Sn, ALL, S(a, b)), True, False)
+                mm(nxt, neg, R(Sn, ALL, S(a + 1, b + 1)), False, False)
+                mm(nxt, R("Inb"), R("r1", ALL, S(a, b)), False, True)
+                act(R("V", ALL, S(a, b)), nxt)
+        else:
+            act(R("pv", ALL, S(p0, p0 + w + 1)), R(Sn, ALL, S(a - 1, b)))
+            tt(R("A", ALL, S(p0, p0 + w)), R("pv", ALL, S(p0, p0 + w)), R(Sn, ALL, S(a + 1, b + 1)), ALU.max)
+            tt(R("V", ALL, S(a, b)), R("pv", ALL, S(p0 + 1, p0 + w + 1)), R("A", ALL, S(p0, p0 + w)), ALU.subtract)
+
+    def rows_split(t):
+        qf = R("pa", ALL, S(256, 512))
+        cp(R("Qf"), R("Q%d" % t))
+        act(R("HL", ALL, S(0, 256)), R("Qf"))
+        act(qf, R("HL", ALL, S(0, 256)))
+        tt(R("HL", ALL, S(256, 512)), R("Qf"), qf, ALU.subtract)
+
+    def rows_pe(r):
+        o = R("pv", ALL, S(256 * (r % 8), 256 * (r % 8) + 256))
+        mm(o, R("Ym", ALL, S(144 * r + 1, 144 * r + 129)), R("HL", ALL, S(0, 256)), True, False)
+        mm(o, R("Ym", ALL, S(144 * r, 144 * r + 128)), R("HL", ALL, S(256, 512)), False, True)
+
+    def rows_act(r):
+        act(R("Rw", ALL, S(r, W, 16)), R("pv", ALL, S(256 * (r % 8), 256 * (r % 8) + 256)))
+
+    K = float(2 ** 27)
+
+    def moved(t):
+        for j in range(4):
+            for B in (2 * j, 2 * j + 1):
+                src = G(R("V"), R("it16", ALL, S(96 * B + 32 * t, 96 * B + 32 * t + 32)))
+                out = R("Vg", ALL, S(512 * B, 512 * B + 512))
+                if OPT["ve"][t][B] == "a":
+                    act(out, src, AF.Sign, bias=2.0 ** -40)
+                else:
+                    ts(out, src, 0.0, -15.0 / 32, ALU.is_ge, ALU.add)
+            for r in range(16):
+                mm(R("pa", ALL, S(64 * j, 64 * j + 64)), R("Z2", ALL, S(32 - 2 * r, 160 - 2 * r)),
+                   R("Vg", ALL, S(1024 * j + r, 1024 * j + 1024, 16)), r == 0, r == 15)
+                if r == 0:
+                    for B in (2 * j, 2 * j + 1):
+                        if OPT["ve"][t][B] == "a":
+                            mm(R("pa", ALL, S(32 * B, 32 * B + 32)), R("Ib"), R("kb"), False, False)
+
+    def rows():
+        for r in range(0, 16, 2):
+            rows_pe(r)
+            rows_pe(r + 1)
+            rows_act(r)
+            rows_act(r + 1)
+
+    def back(lo, hi, step=1):
+        return S(hi - 1, lo - 1 if lo else None, -step)
+
+    def nearest(t):
+        tr(R("Xc"), R("pa", ALL, S(0, 256)))
+        for v in range(2):
+            e = 256 * t + v
+            scan(R("Wn", ALL, S(v, 256, 2)), R("Xc", ALL, S(v, 256, 2)), R("E", ALL, S(e, e + 255, 2)), -BIG, ALU.max, ALU.min)
+            scan(R("Wn", ALL, back(256 + v, 511 + v, 2)), R("Xc", ALL, back(v, 255 + v, 2)), R("En", ALL, back(e, e + 255, 2)),
+                 -BIG, ALU.max, ALU.min)
+        tr(R("C1"), R("Wn", ALL, S(224, 288)))
+        scan(R("C2", ALL, S(1, 32)), R("C1", ALL, S(0, 31)), R("C1", ALL, S(0, 31)), -BIG, ALU.max, ALU.max)
+        scan(R("C2", ALL, back(32, 63)), R("C1", ALL, back(33, 64)), R("C1", ALL, back(33, 64)), -BIG, ALU.max, ALU.max)
+        tr(R("C3"), R("C2"))
+        for v in range(2):
+            ts(R("W1", ALL, S(8, 16), S(16 * v, 16 * v + 16)), R("Wn", ALL, S(256 + v, 512, 2)), R("C3", ALL, S(32 + v, 33 + v)),
+               -1.0, ALU.max, ALU.mult)
+        for v in range(2):
+            ts(R("W1", ALL, S(0, 8), S(16 * v, 16 * v + 16)), R("Wn", ALL, S(v, 256, 2)), R("C3", ALL, S(30 + v, 31 + v)),
+               None, ALU.max)
+        H = OPT["halves"]
+        nb = 8 // H
+        hs = [(S(32 * nb * h, 32 * nb * (h + 1)), S(256 + 32 * nb * h, 256 + 32 * nb * (h + 1)),
+               R("W1", ALL, S(nb * h, nb * (h + 1)), ALL), R("W1", ALL, S(8 + nb * h, 8 + nb * (h + 1)), ALL)) for h in range(H)]
+        tmp = lambda c: R("pb" if c.start else "pt", ALL, c)
+        for c, c2, L, Rr in hs:
+            tt(tmp(c), R("pk", ALL, c), Rr, ALU.subtract)
+        for c, c2, L, Rr in hs:
+            tt(tmp(c), tmp(c), L, ALU.subtract)
+        for c, c2, L, Rr in hs:
+            ts(tmp(c), tmp(c), -1.0, K, ALU.add, ALU.mult)
+        for c, c2, L, Rr in hs:
+            tt(tmp(c), tmp(c), L, ALU.max)
+        for c, c2, L, Rr in hs:
+            tt(R("ch", ALL, c), tmp(c), Rr, ALU.min)
+        for c, c2, L, Rr in hs:
+            ts(R("ee", ALL, c), R("ch", ALL, c), 8191, None, ALU.bitwise_and)
+        for B in range(8):
+            tr(R("en", ALL, S(B, 256, 8)), R("ee", ALL, S(32 * B, 32 * B + 32)))
+        top, loc = S(160, 256), S(0, 160)
+        tt(R("su", ALL, top), R("pk", ALL, S(416, 512)), R("en", ALL, top), ALU.add)
+        tt(R("su", ALL, loc), R("pk", ALL, S(256, 416)), R("en", ALL, loc), ALU.add)
+        ts(R("s16", ALL, top), R("su", ALL, top), 4095.0, None, ALU.min)
+        ts(R("s16", ALL, loc), R("su", ALL, loc), 4095.0, None, ALU.min)
+
+    dst, pieces, qeng = route(T, topo, rank)
+    _d, inpieces, inq = route(T, topo, (rank - 1) % N)
+
+    def send_two(t):
+        moves, reads = [], []
+        for i in (0, 1):
+            a, b, relay, eng = pieces[i]
+            rid, pid, _s = topo.addr(dst if relay is None else relay)
+            in_ = R("Ts0" if t == 0 else "Ts", ALL, S(a, b))
+            reads.append(in_)
+            moves.append(RemoteDMATransfer(dst_ids=[DstId(rid=rid, pnc=pid)], dma_engine_mask=bits(eng),
+                                           remote_sem=T.sem["r%d" % (4 * t + i)] if relay is None else T.sem["h%d" % t],
+                                           src=in_[2], dst=T["L%d" % t][:, a:b]))
+        s = "s%d" % (4 * t)
+        return op("r", lambda: g.remote_dma_fused(moves, local_sem=T.sem[s]), [], reads, sem=s,
+                  inc=len(pieces[0][3]) + len(pieces[1][3]), cost=0.8, lat=OPT["rlat"][1])
+
+    def send(t, i):
+        if i < len(pieces):
+            a, b, relay, eng = pieces[i]
+            to = dst if relay is None else relay
+            out, in_ = R("L%d" % t, ALL, S(a, b)), R("Ts0" if t == 0 else "Ts", ALL, S(a, b))
+            rs = T.sem["r%d" % (4 * t + i)] if relay is None else T.sem["h%d" % t]
+        else:
+            to, eng = dst, qeng
+            out, in_ = R("Q%d" % t, ALL, S(0, 96)), R("Qs", ALL, S(96 * t, 96 * t + 96))
+            rs = T.sem["r%d" % (4 * t + i)]
+        rid, pid, _s = topo.addr(to)
+        s = "s%d" % (4 * t + i)
+        return op("r", lambda: g.remote_dma(out[2], in_[2], rs, T.sem[s], pid, rid, bits(eng)), [], [in_], sem=s,
+                  inc=len(eng), cost=0.8, lat=OPT["rlat"][i])
+
+    def arrive(t, sent):
+        for i, (a, b, relay, eng) in enumerate(inpieces):
+            n = len(eng) if relay is None else len(topo.engines(relay, core))
+            op("x", None, [R("L%d" % t, ALL, S(a, b))], [], sem="r%d" % (4 * t + i), inc=n,
+               cost=OPT["rlat"][0] if i == 0 else 0.0, after=[sent[i]])
+        op("x", None, [R("Q%d" % t, ALL, S(0, 96))], [], sem="r%d" % (4 * t + len(inpieces)), inc=len(inq), cost=0.0,
+           after=[sent[-1]])
+
+    def gath(q, out, win, off):
+        if q == "a":
+            act(out, G(win, off))
+        else:
+            cp(out, G(win, off))
+
+    def rgath(q, k0, k1):
+        gath(q, R("Vg", ALL, S(16 * k0, 16 * k1)), R("Rw"), R("s16", ALL, S(k0, k1)))
+
+    def rpick(t, k0, k1, bank):
+        o = R(bank, ALL, S(k0, k1))
+        turn = t == 0 and k0 < 160
+        z = 16 if turn else 32
+        for r in range(16):
+            mm(o, R("Z", ALL, S(z - r, z + 128 - r)), R("Vg", ALL, S(16 * k0 + r, 16 * k1, 16)), r == 0, r == 15 and not turn)
+        if turn:
+            mm(o, R("Iw", ALL, S(0, 128)), R("hd", ALL, S(k0, k1)), False, True)
+
+    def qlist(t, k0, k1, bank):
+        c = S(k0, k1)
+        if t == 0 and k0 < 160:
+            cp(R("Qx", ALL, c), R(bank, ALL, c))
+        else:
+            tt(R("Qx", ALL, c), R(bank, ALL, c), R("hd", ALL, c), ALU.add)
+        ts(R("Qi", ALL, c), R("Qx", ALL, c), 4095, None, ALU.bitwise_and)
+        if k0 < 160:
+            cp(R("Q%d" % t, ALL, S(96 + k0, 96 + k1)), R("Qi", ALL, c))
+        else:
+            cp(R("Qs", ALL, S(96 * t + k0 - 160, 96 * t + k1 - 160)), R("Qi", ALL, c))
+
+    def shift(t):
+        old = ("spb", "Sx", "Sy")[t]
+        new = ("Sx", "Sy", "Sx")[t]
+        lwin = R("spa") if t == 0 else R(old, ALL, S(0, W))
+        if t == 0:
+            mm(R("pb", ALL, S(0, 160)), R("Iw", ALL, S(0, 128)), R("su", ALL, S(0, 160)), True, True)
+            ts(R("s16a"), R("pb", ALL, S(0, 160)), 4095.0, None, ALU.min)
+        sent = []
+        for i, (a, b, _r, _e) in enumerate(pieces):
+            gath(OPT["te"][t][i], R("Ts0" if t == 0 else "Ts", ALL, S(a, b)), R(old, ALL, S(0, W)),
+                 R("s16", ALL, S(160 + a // 16, 160 + b // 16)))
+            if i == 1:
+                sent += [send_two(t)] * 2
+            if i == 2:
+                sent.append(send(t, i))
+        if OPT["hd"] == "v":
+            ts(R("hd"), R("en"), -4096.0, R("nh", ALL, S(t, t + 1)), ALU.add, ALU.mult)
+        else:
+            e = R("pa", ALL, S(256, 512))
+            mm(e, R("Iw", ALL, S(16, 144)), R("su"), True, False)
+            mm(e, R("In"), R("mS"), False, True)
+            nh = R("nh", ALL, S(t, t + 1))
+            op("a", lambda: g.scalar.activation(T.hd[:], e[2], AF.Copy, scale=nh[2]), [R("hd")], [e, nh])
+        for q, k0, k1 in OPT["rt"][t]:
+            rgath(q, k0, k1)
+        rpick(t, 160, 256, "pa")
+        qlist(t, 160, 256, "pa")
+        sent.append(send(t, len(pieces)))
+        arrive(t, sent)
+
+        def mul(a, b):
+            rec = "recb" if (t == 2 and a < X) else "reca"
+            other = R("L%d" % t, ALL, S(a, b)) if a < X else R("Tl", ALL, S(a - X, b - X))
+            tt(R(new, ALL, S(a, b)), G(R(rec), R("Q%d" % t, ALL, S(a // 16, b // 16))), other, ALU.mult)
+
+        nr, nv, lc = 0, 0, OPT["lc"]
+        for what, q, k0, k1 in OPT["loc"][t]:
+            if what == "R":
+                rgath(q, k0, k1)
+                rpick(t, k0, k1, "pb" if nr % 2 == 0 else "pt")
+                qlist(t, k0, k1, "pb" if nr % 2 == 0 else "pt")
+                nr += 1
+                continue
+            gath(q, R("Tl", ALL, S(16 * k0, 16 * k1)), lwin, R("s16a" if t == 0 else "s16", ALL, S(k0, k1)))
+            mul(X + 16 * k0, X + 16 * k1)
+            while t < 2 and nv < len(lc) - 1 and (lc[nv + 1] < X + 16 * k1 - OPT["lag"] or k1 == 160):
+                votes(new, lc[nv], lc[nv + 1], OPT["lmode"][nv])
+                nv += 1
+        if t < 2:
+            rows_split(t)
+        if t == 2:
+            for j in range(3):
+                mm(R("pv", ALL, S(512 * j, 512 * j + 512)), R("Iw", ALL, S(32, 160)),
+                   R(new, ALL, S(2048 + 512 * j, 2560 + 512 * j)), True, j >= OPT["pj"])
+            o = R("pv", ALL, S(X, 2048))
+            mm(o, R("Iw", ALL, S(16, 144)), R(new, ALL, S(X, 2048)), True, False)
+            mm(o, R("Iw", ALL, S(16, 144)), R(new, ALL, S(3584, W)), False, True)
+            act(R("Yo", ALL, S(X, 2048)), o)
+            store("ss", S(X, 2048), rank)
+        for j in range(3):
+            mul(512 * j, 512 * j + 512)
+            if t == 2:
+                c = S(512 * j, 512 * j + 512)
+                if j < OPT["pj"]:
+                    mm(R("pv", ALL, c), R("Iw", ALL, S(16, 144)), R(new, ALL, c), False, True)
+                    act(R("Yo", ALL, c), R("pv", ALL, c))
+                else:
+                    tt(R("Yo", ALL, c), R("pv", ALL, c), R(new, ALL, c), ALU.add)
+                store("ss" if j < 2 else "sa", c, rank + 1)
+        if t < 2:
+            rc = OPT["rc"]
+            for j in range(len(rc) - 1):
+                votes(new, rc[j], rc[j + 1], OPT["rmode"][j])
+
+    def store(q2, c, k):
+        k %= 8
+        dma(q2[0], R("y", S(16 * k, 128), c), R("Yo", S(0, 128 - 16 * k), c), False)
+        if k:
+            dma(q2[1], R("y", S(0, 16 * k), c), R("Yo", S(128 - 16 * k, 128), c), False)
+
+    cuts = OPT["c0"]
+    lists(0, 1)
+    for i in range(len(cuts) - 1):
+        votes("spb", cuts[i], cuts[i + 1], OPT["m0"][i])
+    first_rows()
+    turned("ss", "recb", ALL, "rec", ALL, rank + 1)
+    for t in range(3):
+        if t == 1:
+            lists(1, 3)
+        moved(t)
+        if t == 0:
+            keys_a(0, 1)
+            late()
+            hops()
+        if t == 1:
+            keys_a(1, 3)
+        keys(t)
+        nearest(t)
+        if t > 0:
+            rows()
+        shift(t)
+
+    n = len(ops)
+    succ = [[] for _ in range(n)]
+    pred = [[] for _ in range(n)]
+    for i, o in enumerate(ops):
+        for d in o["deps"] | o["order"]:
+            gap = ops[d]["lat"] + OPT["wake"] if d in o["deps"] or o["q"] == "x" else 0.0
+            succ[d].append((i, gap))
+            pred[i].append((d, gap))
+    lanes = ["p" if o["q"] == "r" else o["q"] for o in ops]
+    lane = lambda i: lanes[i]
+    cost = [o["cost"] for o in ops]
+
+    def lay(prio, nxt, prv, ready, slack):
+        left = [len(p) for p in prv]
+        pools = {}
+        for i in range(n):
+            if not left[i]:
+                pools.setdefault(lanes[i], []).append(i)
+        free, out, ends = {}, [], [0.0] * n
+        while len(out) < n:
+            first, q = min((max(min(ready[i] for i in p), free.get(k, 0.0)), k) for k, p in pools.items() if p)
+            i = max((j for j in pools[q] if ready[j] <= first + (OPT["tslack"] if q == "t" else slack)), key=lambda j: (prio[j], -j))
+            pools[q].remove(i)
+            out.append(i)
+            ends[i] = max(ready[i], free.get(q, 0.0)) + cost[i]
+            if q != "x":
+                free[q] = ends[i]
+            for j, gap in nxt[i]:
+                ready[j] = max(ready[j], ends[i] + gap)
+                left[j] -= 1
+                if not left[j]:
+                    pools.setdefault(lanes[j], []).append(j)
+        return out, ends
+
+    tail = [0.0] * n
+    for i in range(n - 1, -1, -1):
+        tail[i] = cost[i] + max([ops[i]["lat"]] + [tail[j] + gap for j, gap in succ[i]])
+    best = None
+    rng = np.random.default_rng(1)
+    prio = [-float(i) for i in range(n)]
+    for k in range(OPT["tries"]):
+        out, ends = lay(prio, succ, pred, [0.0] * n, OPT["slack"])
+        span = max(ends[i] + ops[i]["lat"] for i in range(n))
+        if best is None or span < best[0]:
+            best = (span, out, ends)
+        base = ends if k % 4 != 3 else best[2]
+        noise = rng.random(n) * OPT["noise"] * (k % 4 == 3)
+        _o, prio = lay([float(e + z) for e, z in zip(base, noise)], pred, succ, [o["lat"] for o in ops], OPT["slack"])
+    seq = best[1]
+    SPAN[rank] = best[0]
+    place = {i: k for k, i in enumerate(seq)}
+    need = set()
+    for o in ops:
+        latest = {}
+        for d in o["deps"]:
+            k = ops[d]["sem"] or ops[d]["q"]
+            if k not in latest or place[d] > place[latest[k]]:
+                latest[k] = d
+        o["deps"] = set(latest.values())
+        need |= o["deps"]
+    count = {}
+    mark = [None] * n
+    for i in seq:
+        o = ops[i]
+        if o["sem"] is not None:
+            mark[i] = (o["sem"], o["inc"])
+        elif i in need:
+            count[o["q"]] = count.get(o["q"], 0) + 1
+            mark[i] = (o["q"], count[o["q"]])
+    known = {}
+    clock = [None] * n
+    for i in seq:
+        o = ops[i]
+        if o["q"] == "x":
+            clock[i] = {}
+            continue
+        q = lane(i)
+        kn = known.setdefault(q, {})
+        for d in sorted(o["deps"], key=lambda d: -place[d]):
+            s, val = mark[d]
+            if kn.get(s, 0) < val:
+                Q[q].wait_ge(T.sem[s], val)
+                kn[s] = val
+                for s2, v2 in clock[d].items():
+                    if kn.get(s2, 0) < v2:
+                        kn[s2] = v2
+        clock[i] = dict(kn)
+        ins = o["fn"]()
+        if mark[i] is not None and o["q"] != "r":
+            ins.then_inc(T.sem[mark[i][0]], o["inc"])
+    total = {}
+    for m in mark:
+        if m is not None:
+            total[m[0]] = max(total.get(m[0], 0), m[1])
+    for s, val in total.items():
+        if not any(kn.get(s, 0) >= val for kn in known.values()):
+            g.sync.wait_ge(T.sem[s], val)

@@ -11,49 +11,56 @@ SCRATCH = {
     "Tl": ("sbuf", [128, LOC], F32), "Ts": ("sbuf", [128, X], F32), "Ts0": ("sbuf", [128, X], BF),
     "L0": ("sbuf", [128, X], BF), "L1": ("sbuf", [128, X], F32), "L2": ("sbuf", [128, X], F32),
     "V": ("sbuf", [128, W], BF), "Vg": ("sbuf", [128, W], BF), "Rw": ("sbuf", [128, W], BF),
-    "r2": ("sbuf", [128, W], BF), "mS": ("sbuf", [128, 256], F32), "r1": ("sbuf", [128, W], BF), "A": ("sbuf", [128, 2048], F32),
+    "mS": ("sbuf", [128, 256], F32), "r1": ("sbuf", [128, 2048], BF), "r2": ("sbuf", [128, 2048], BF),
     "Yo": ("sbuf", [128, 2048], F32),
     "Q0": ("sbuf", [128, 256], U16), "Q1": ("sbuf", [128, 256], U16), "Q2": ("sbuf", [128, 256], U16),
     "Qs": ("sbuf", [128, 288], U16), "Qi": ("sbuf", [128, 256], I32), "Qx": ("sbuf", [128, 256], I32),
-    "Qf": ("sbuf", [128, 256], F32), "HL": ("sbuf", [128, 512], BF),
-    "it": ("sbuf", [128, 768], I32), "it16": ("sbuf", [128, 768], U16), "itT": ("sbuf", [128, 8, 96], I32),
-    "E": ("sbuf", [128, 768], F32), "En": ("sbuf", [128, 768], F32),
-    "cI": ("sbuf", [128, 8, 32], F32), "Xc": ("sbuf", [128, 256], F32), "Z2": ("sbuf", [128, 160], BF),
-    "Wn": ("sbuf", [128, 512], F32), "W1": ("sbuf", [128, 16, 32], F32),
-    "C1": ("sbuf", [128, 64], F32), "C2": ("sbuf", [128, 64], F32), "C3": ("sbuf", [128, 64], F32),
-    "tt": ("sbuf", [128, 256], F32), "ch": ("sbuf", [128, 256], I32), "ee": ("sbuf", [128, 256], I32),
+    "Qf": ("sbuf", [128, 256], F32), "HL": ("sbuf", [128, 256], BF),
+    "it": ("sbuf", [128, 768], I32), "it16": ("sbuf", [128, 768], U16),
+    "E": ("sbuf", [128, 768], F32), "En": ("sbuf", [128, 768], F32), "Z2": ("sbuf", [128, 160], BF),
+    "Xc": ("sbuf", [128, 256], F32), "Xn": ("sbuf", [128, 256], F32),
+    "Wf": ("sbuf", [128, 256], F32), "Wb": ("sbuf", [128, 256], F32),
+    "Et": ("sbuf", [128, 256], F32), "Lf": ("sbuf", [128, 256], F32), "Lb": ("sbuf", [128, 256], F32),
+    "Lk": ("sbuf", [128, 256], F32), "Rk": ("sbuf", [128, 256], F32), "c2": ("sbuf", [128, 256], F32),
+    "Bs": ("sbuf", [128, 2, 128], F32), "IK": ("sbuf", [128, 128], F32),
+    "ch": ("sbuf", [128, 256], I32),
     "en": ("sbuf", [128, 256], I32), "su": ("sbuf", [128, 256], F32), "hd": ("sbuf", [128, 256], F32),
     "s16": ("sbuf", [128, 256], U16), "s16a": ("sbuf", [128, 160], U16),
     "rs": ("sbuf", [128, 256], I32), "hrow": ("sbuf", [128, 32], I32), "hb": ("sbuf", [128, 32], I32),
     "hm": ("sbuf", [128, 24], F32), "nh": ("sbuf", [128, 4], F32),
     "i1": ("sbuf", [128, 160], I32), "i2": ("sbuf", [128, 160], I32), "i3": ("sbuf", [128, 160], I32),
-    "pc": ("sbuf", [128, 4], I32), "pm": ("sbuf", [128, 4], I32), "pf": ("sbuf", [128, 4], F32),
+    "i4": ("sbuf", [128, 8], I32),
+    "pc": ("sbuf", [128, 4], I32), "pm": ("sbuf", [128, 8], I32), "pf": ("sbuf", [128, 8], F32),
     "kb": ("sbuf", [128, 32], BF), "mk": ("sbuf", [128, 256], F32),
     "Iw": ("sbuf", [128, 160], F32), "In": ("sbuf", [128, 128], F32), "Ib": ("sbuf", [128, 128], BF),
-    "Inb": ("sbuf", [128, 128], BF), "Z": ("sbuf", [128, 160], BF), "Ym": ("sbuf", [128, 2304], BF),
+    "Inb": ("sbuf", [128, 128], BF), "Z": ("sbuf", [128, 160], BF),
+    "Sw": ("sbuf", [128, 2, 128], F32), "Sb": ("sbuf", [128, 2, 128], BF), "Pm": ("sbuf", [128, 8], F32),
     "pv": ("psum", [128, 2048], F32), "pa": ("psum", [128, 512], F32), "pb": ("psum", [128, 512], F32),
     "pk": ("psum", [128, 512], F32), "pt": ("psum", [128, 512], F32),
 }
 NDMA = 48
 SEMAPHORES = ["v", "a", "t", "p", "sent"] + ["d%d" % i for i in range(NDMA)] + ["s%d" % i for i in range(12)] + \
     ["r%d" % i for i in range(12)] + ["h%d" % i for i in range(6)]
-ROWED = ("spa", "spb", "reca", "recb", "it", "rs", "Rw", "hrow", "cI", "y")
+ROWED = ("spa", "spb", "reca", "recb", "it", "rs", "hrow", "y")
 BIG = float(2 ** 26)
-P5 = [0, 32, 64, 96, 128, 160]
+K = float(2 ** 27)
 SPAN = {}
-LOC01 = [("R", "v", 0, 32), ("T", "a", 0, 32), ("R", "a", 32, 96), ("R", "a", 96, 160), ("T", "a", 32, 64),
-         ("T", "a", 64, 96), ("T", "a", 96, 128), ("T", "a", 128, 160)]
-LOC2 = [("R", "a", 0, 64), ("R", "a", 64, 128), ("T", "a", 0, 32), ("R", "a", 128, 160), ("T", "a", 32, 64),
-        ("T", "a", 64, 96), ("T", "a", 96, 128), ("T", "a", 128, 160)]
-OPT = {"hd": "a", "pj": 0, "tslack": 0.0, "tries": 1, "noise": 1.0, "relay": True, "halves": 2, "strict": False,
-       "pe": 0.45e-3, "gat": 1.56, "dbw": 400e3, "wake": 0.08, "slack": 0.0,
-       "rlat": (4.0, 6.0, 8.0, 5.0), "m0": "qpqpqpqppp",
+CELLS = {}
+P01 = ("Rv160-224 Ha Rv224-256 Ta0 Ta1 Ta2 Ra0-64 Q-160-256 X M-1024-1536 Lv0 Rv64-96 Q-0-64 M-1536-2048 Lv2 Ra96-160 La1 La3 "
+       "M-512-1024 M-2048-2560 La4 Q-64-96 Q-96-160 M-3072-3584 M-0-512 M-3584-4096 M-2560-3072 Dz1537-2047 Da2047-2558 "
+       "Da3580-3840 Dz2558-3069 Wz1537-2047 Wa2047-2558 Wz2558-3069 Wa3580-3840 Da511-1022 Dz3840-4096 Wz3840-4096 Da1-511 "
+       "Dz1280-1537 Da3069-3580 Wa511-1022 S Dp1022-1280 Wz1280-1537 Wa1-511 Wa3069-3580 Wp1022-1280")
+P2 = ("Ta0 Ta1 Rv160-256 Ha Ra96-160 Ra32-64 Tv2 Rv64-96 Ra0-32 La0 Q-160-256 Q-0-96 La3 Q-96-160 La4 X La2 La1 M-2560-3072 "
+      "M-0-512 Uv512-1024 M-1280-1536 M-1536-2048 M-3584-4096 M-2048-2560 Uv1536-2048 M-3072-3584 Uv1024-1536 Ua0-512 "
+      "M-512-1024 M-1024-1280 Yv512-1024 Yv1536-2048 Ya0-512 Yv1280-1536 Yv1024-1280")
+OPT = {"greedy": True, "slack": {"v": 0.1, "a": 0.1, "t": 0.1}, "fit": 0.0, "relay": True,
+       "parts": [[(160, 256), (0, 160)]] * 3, "ilv": [[(0,), (1,)]] * 3,
+       "pe": 0.46e-3, "cy": 0.86e-3, "fix": 0.025, "gat": 1.45, "dbw": 500e3, "wake": 0.19,
+       "rlat": (4.0, 5.5, 6.5, 4.5), "m0": "pcppppppq",
        "sp": [0, 1024, 2560, 4096],
-       "c0": [1, 512, 1023, 1534, 2045, 2556, 3067, 3578, 3840, 4096], "rc": [1, 511, 1022, 1280, 1537],
-       "lc": [1537, 2047, 2558, 3069, 3580, 3840, 4096], "lag": 512,
-       "lmode": "zazaza", "rmode": "zaaa", "ve": ["avavavav"] * 3, "te": ["ava"] * 3,
-       "rt": [[("v", 160, 256)]] * 3,
-       "loc": [LOC01, LOC01, LOC2]}
+       "c0": [1, 512, 1023, 1534, 2045, 2556, 3067, 3578, 3840, 4096],
+       "ve": ["vavaavav", "avavavav", "avavavav"], "plan": [P01, P01, P2],
+       "pre": "1 cnt 0 row split 3 4 5 key lists 6 2 8 7 moved keys hops late"}
 
 
 def route(T, topo, rank):
@@ -103,7 +110,6 @@ def rank_program(g, core, T, topo):
     ops = []
     shapes = {k: v[1] for k, v in SCRATCH.items()}
     shapes["y"] = [128, 2048]
-    grid = {}
     last_w = {}
     readers = {}
 
@@ -116,21 +122,15 @@ def rank_program(g, core, T, topo):
 
     def cells(ref):
         name, idx = ref[0], ref[1]
-        sh = shapes[name]
-        if name not in grid:
-            n = int(np.prod(sh[1:]))
-            rows = 128 if name in ROWED else 1
-            grid[name] = np.arange(rows * n).reshape([rows] + list(sh[1:]))
-            last_w[name] = np.full(rows * n, -1, np.int32)
-            readers[name] = []
-        if name in ROWED:
-            c = grid[name][idx].ravel()
-        else:
-            c = grid[name][(slice(None),) + tuple(idx[1:])].ravel()
-        if SCRATCH.get(name, ("", ))[0] == "psum":
-            b = np.unique(c // 512)
-            c = (b[:, None] * 512 + np.arange(512)[None, :]).ravel()
-        return name, c
+        key = (name, repr(idx))
+        if key not in CELLS:
+            m = np.zeros(shapes[name], bool)
+            m[idx] = True
+            m = m.reshape(8, 16, -1).any(axis=1) if name in ROWED else m.reshape(128, -1).any(axis=0)
+            if SCRATCH.get(name, ("", ))[0] == "psum":
+                m = m.reshape(-1, 512).any(axis=1)
+            CELLS[key] = int.from_bytes(np.packbits(m.ravel()).tobytes(), "big")
+        return name, CELLS[key]
 
     def flat(refs):
         out = []
@@ -153,13 +153,15 @@ def rank_program(g, core, T, topo):
             return max(64, width(writes[0])) * OPT["pe"] * (4 if SCRATCH[full[0][0]][2] == F32 else 1)
         n = width(writes[0])
         if any(isinstance(r[0], tuple) for r in full):
-            return 0.055 + n * OPT["gat"] * 0.83e-3
+            return 0.055 + n * OPT["gat"] * OPT["cy"]
         if q == "p":
-            return 0.15 + n * 1.66e-3
+            return 0.15 + n * 2 * OPT["cy"]
         big = [r for r in full if width(r) == n]
         if len(big) == 2 and all(SCRATCH[r[0]][0] == "sbuf" for r in big) and n > 1:
             n *= 2
-        return 0.03 + max(64, n) * 0.83e-3
+        elif q == "v" and all(SCRATCH[r[0]][2] in (BF, U16) for r in big + writes):
+            n //= 2
+        return OPT["fix"] + max(64, n) * OPT["cy"]
 
     def op(q, fn, writes, reads, sem=None, inc=1, cost=None, lat=0.0, after=()):
         me = len(ops)
@@ -170,32 +172,19 @@ def rank_program(g, core, T, topo):
                 continue
             name, c = cells(r)
             psum = SCRATCH.get(name, ("", ))[0] == "psum"
-            for d in np.unique(last_w[name][c]):
-                if d >= 0:
-                    deps.add(int(d))
+            deps.update(d for d, cc in last_w.get(name, []) if cc & c)
             if psum:
-                for (d, cc) in readers[name]:
-                    if ops[d]["q"] != q and np.any(cc[c]):
-                        deps.add(d)
-            m = np.zeros(last_w[name].size, bool)
-            m[c] = True
-            readers[name].append((me, m))
+                deps.update(d for d, cc in readers.get(name, []) if ops[d]["q"] != q and cc & c)
+            readers.setdefault(name, []).append((me, c))
         for r in flat(writes):
             name, c = cells(r)
-            psum = SCRATCH.get(name, ("", ))[0] == "psum"
-            for d in np.unique(last_w[name][c]):
-                if d >= 0:
+            for d, cc in last_w.get(name, []):
+                if cc & c:
                     same = ops[d]["q"] == q and sem is None and ops[d]["sem"] is None
-                    (order if same and q == "t" else deps).add(int(d))
-            keep = []
-            for (d, cc) in readers[name]:
-                if d != me and np.any(cc[c]):
-                    deps.add(d)
-                    cc[c] = False
-                if np.any(cc):
-                    keep.append((d, cc))
-            readers[name] = keep
-            last_w[name][c] = me
+                    (order if same and q == "t" else deps).add(d)
+            deps.update(d for d, cc in readers.get(name, []) if cc & c)
+            readers[name] = [(d, cc & ~c) for d, cc in readers.get(name, []) if cc & ~c]
+            last_w[name] = [(d, cc & ~c) for d, cc in last_w.get(name, []) if cc & ~c] + [(me, c)]
         deps.discard(me)
         if cost is None:
             cost = price(q, writes, reads)
@@ -218,7 +207,7 @@ def rank_program(g, core, T, topo):
         if load:
             moved_us[0] += us
             us = moved_us[0]
-        op(q, lambda: Q[q].dma_start(out[2], in_[2]), [out], [in_], sem=s, inc=16, cost=0.1, lat=2.0 + us)
+        op(q, lambda: Q[q].dma_start(out[2], in_[2]), [out], [in_], sem=s, inc=16, cost=0.06, lat=1.8 + us)
 
     def ap(x):
         return x[2] if isinstance(x, tuple) else x
@@ -240,16 +229,16 @@ def rank_program(g, core, T, topo):
 
     def scan(out, d0, d1, init, o0, o1):
         op("v", lambda: g.vector.tensor_tensor_scan(out[2], d0[2], d1[2], init, o0, o1), [out], [d0, d1],
-           cost=0.03 + max(64, width(out)) * 0.83e-3)
+           cost=OPT["fix"] + max(64, width(out)) * OPT["cy"])
 
     def fill(out, c):
         op("v", lambda: g.vector.memset(out[2], c), [out], [])
 
     def act(out, a, f=AF.Copy, bias=0.0, scale=1.0):
         if f == AF.Copy:
-            op("a", lambda: g.scalar.activation(out[2], a[2], f, scale=scale), [out], [a])
+            op("a", lambda: g.scalar.activation(out[2], a[2], f, scale=ap(scale)), [out], [a, scale])
         else:
-            op("a", lambda: g.scalar.activation(out[2], a[2], f, bias=bias, scale=scale), [out], [a])
+            op("a", lambda: g.scalar.activation(out[2], a[2], f, bias=ap(bias), scale=ap(scale)), [out], [a, bias, scale])
 
     def mm(out, l, r, start, stop):
         op("t", lambda: g.tensor.matmul(out[2], l[2], r[2], start, stop), [out], [l, r])
@@ -262,79 +251,86 @@ def rank_program(g, core, T, topo):
 
     S = slice
     ALL = S(None)
+    col = lambda name, k: R(name, ALL, S(k, k + 1))
 
     def turned(q2, buf, cols, src, scols, k, unit=16):
         k %= 8
-        dma(q2[0], R(buf, S(0, 128 - 16 * k), cols), (src, None, T[src][unit * k:unit * 8, scols]))
+        dma(q2[0], R(buf, S(0, 128 - 16 * k), *cols), (src, None, T[src][unit * k:unit * 8, scols]))
         if k:
-            dma(q2[1], R(buf, S(128 - 16 * k, 128), cols), (src, None, T[src][0:unit * k, scols]))
+            dma(q2[1], R(buf, S(128 - 16 * k, 128), *cols), (src, None, T[src][0:unit * k, scols]))
 
     sp = OPT["sp"]
-    turned("ss", "spb", S(sp[0], sp[1]), "sp", S(sp[0], sp[1]), rank + 1)
-    turned("aa", "it", S(0, 256), "itg", S(0, 256), rank + 1)
-    turned("aa", "it", S(256, 768), "itg", S(256, 768), rank)
+    turned("ss", "spb", (S(sp[0], sp[1]),), "sp", S(sp[0], sp[1]), rank + 1)
     for i in range(1, len(sp) - 1):
-        turned("ss", "spb", S(sp[i], sp[i + 1]), "sp", S(sp[i], sp[i + 1]), rank + 1)
-    turned("ss", "rs", ALL, "rot", ALL, rank + 1, unit=1)
+        turned("ss", "spb", (S(sp[i], sp[i + 1]),), "sp", S(sp[i], sp[i + 1]), rank + 1)
+    turned("ss", "it", (S(0, 256),), "itg", S(0, 256), rank + 1)
+    turned("ss", "rs", (ALL,), "rot", ALL, rank + 1, unit=1)
+    turned("ss", "it", (S(256, 768),), "itg", S(256, 768), rank)
     dma("s", R("hrow", S(0, 1), S(0, 3 * (8 - rank))), ("hop", None, T.hop[rank:8, :]))
     dma("s", R("hrow", S(0, 1), S(3 * (8 - rank), 27)), ("hop", None, T.hop[0:rank + 1, :]))
-    turned("ss", "spa", ALL, "sp", ALL, rank)
-    turned("ss", "reca", ALL, "rec", ALL, rank)
+    turned("ss", "spa", (ALL,), "sp", ALL, rank)
+    turned("ss", "reca", (ALL,), "rec", ALL, rank)
+    turned("ss", "recb", (ALL,), "rec", ALL, rank + 1)
 
     iota(R("i1"), [[1, 160]], 112, -1)
     iota(R("pc"), [[0, 4]], 0, 1)
-    fill(R("spb", ALL, S(W, W + 16)), 0.0)
-    ts(R("i2"), R("i1"), 127, None, ALU.bitwise_and)
-    ts(R("pm"), R("pc"), 15, None, ALU.bitwise_and)
-    ts(R("Ib"), R("i2", ALL, S(16, 144)), 0.0, None, ALU.is_equal)
-    ts(R("Inb"), R("i2", ALL, S(16, 144)), 0.0, -1.0, ALU.is_equal, ALU.mult)
-    cp(R("pf"), R("pm"))
-    ts(R("Iw"), R("i2"), 0.0, None, ALU.is_equal)
-    ts(R("In"), R("i2", ALL, S(16, 144)), 0.0, -1.0, ALU.is_equal, ALU.mult)
-    ts(R("i3"), R("i1"), R("pf", ALL, S(0, 1)), 112.0, ALU.add, ALU.add)
-    fill(R("V", ALL, S(0, 1)), 1.0)
-    ts(R("i3"), R("i3"), 127, None, ALU.bitwise_and)
-    fill(R("C2"), -BIG)
-    ts(R("Z"), R("i3"), 0.0, None, ALU.is_equal)
-    ts(R("pm", ALL, S(1, 2)), R("pc", ALL, S(1, 2)), 31, None, ALU.bitwise_and)
-    ts(R("pm", ALL, S(2, 3)), R("pc", ALL, S(2, 3)), 4, 1, ALU.logical_shift_right, ALU.bitwise_and)
-    tt(R("pf", ALL, S(1, 2)), R("pm", ALL, S(1, 2)), R("pm", ALL, S(2, 3)), ALU.subtract)
-    ts(R("Z2"), R("i1"), R("pf", ALL, S(1, 2)), 144.0, ALU.add, ALU.is_equal)
-    ts(R("Z2"), R("Z2"), 2 * BIG, None, ALU.mult)
-    fill(R("kb"), 2 * BIG)
-    fill(R("Sx", ALL, S(W, W + 8)), 0.0)
-    fill(R("Sy", ALL, S(W, W + 8)), 0.0)
-    iota(R("cI"), [[16, 8], [0, 2], [1, 16]], -2048, 128, True)
-    iota(R("mk"), [[16, 256]], -4096, 0, True)
-    iota(R("Rw"), [[0, W]], 0, 0, True)
+    iota(R("spb", ALL, S(W, W + 16)), [[0, 16]], 0, 0, True)
+    iota(R("V", ALL, S(0, 1)), [[0, 1]], 1, 0, True)
+    iota(R("i4"), [[1, 8]], 0, 0)
+    iota(R("mk"), [[16, 256]], -2048, 0, True)
+    iota(R("Sx", ALL, S(W, W + 8)), [[0, 8]], 0, 0, True)
+    iota(R("Sy", ALL, S(W, W + 8)), [[0, 8]], 0, 0, True)
     op("p", lambda: g.partition_broadcast(T.hb[:, 0:27], T.hrow[0:1, 0:27], 128), [R("hb")], [R("hrow", S(0, 1), S(0, 27))])
-    iota(R("Ym"), [[0, 2304]], 1, 0, True)
-    op("p", lambda: g.affine_select(T.Ym[:], T.Ym[:], [[-1, 16], [-16, 9], [1000, 16]], ALU.is_equal, 0.0, -1000, 1),
-       [R("Ym")], [R("Ym")])
-    ts(R("pm", ALL, S(3, 4)), R("pc", ALL, S(3, 4)), 5, None, ALU.logical_shift_right)
-    ts(R("pf", ALL, S(2, 3)), R("pm", ALL, S(3, 4)), -4096.0, None, ALU.mult)
-    ts(R("cI"), R("cI"), R("pf", ALL, S(2, 3)), 8191.0, ALU.add, ALU.mult)
-    ts(R("cI"), R("cI"), 2048.0, None, ALU.add)
+    ts(R("i2"), R("i1"), 127, None, ALU.bitwise_and)
+    ts(R("Ib"), R("i2", ALL, S(16, 144)), 0.0, None, ALU.is_equal)
+    act(R("Inb"), R("Ib"), scale=-1.0)
 
-    def late():
-        ts(R("pk", ALL, S(0, 256)), R("cI"), 2.0, None, ALU.mult)
-        ts(R("pk", ALL, S(256, 512)), R("mk"), R("pf", ALL, S(0, 1)), None, ALU.add)
-        if OPT["hd"] != "v":
-            ts(R("mS"), R("mk"), R("pf", ALL, S(0, 1)), 4096.0, ALU.add, ALU.add)
+    def count_consts():
+        ts(col("pm", 0), col("pc", 0), 15, None, ALU.bitwise_and)
+        cp(col("pf", 0), col("pm", 0))
+        ts(R("i3"), R("i1"), col("pf", 0), 112.0, ALU.add, ALU.add)
+        ts(R("i3"), R("i3"), 127, None, ALU.bitwise_and)
+        ts(R("Z"), R("i3"), 0.0, None, ALU.is_equal)
+        act(R("Z2"), R("Z"), scale=2 * BIG)
+        fill(R("kb"), 2 * BIG)
 
-    def lists(t0, t1):
-        for B in range(8):
-            cp(R("it16", ALL, S(96 * B + 32 * t0, 96 * B + 32 * t1)), R("it", ALL, S(256 * t0 + B, 256 * t1, 8)))
+    def row_consts():
+        ts(R("Iw"), R("i2"), 0.0, None, ALU.is_equal)
+        ts(col("pm", 4), col("pc", 0), 1, None, ALU.bitwise_and)
+        ts(col("pm", 5), col("pc", 0), 1, 7, ALU.logical_shift_right, ALU.bitwise_and)
+        cp(R("pf", ALL, S(4, 6)), R("pm", ALL, S(4, 6)))
+        ts(col("pf", 3), col("pf", 4), -1.0, 1.0, ALU.mult, ALU.add)
+        ts(R("Pm"), R("i4"), col("pf", 5), None, ALU.is_equal)
+        for v in range(2):
+            act(R("Sw", ALL, v, ALL), R("Iw", ALL, S(15 + 2 * v, 143 + 2 * v)), scale=col("pf", 3 + v))
+            act(R("pt", ALL, S(256 + 128 * v, 384 + 128 * v)), R("Iw", ALL, S(16, 144)), scale=col("pf", 3 + v))
+        tt(R("Sb"), R("pt", ALL, S(256, 512)), R("Sw"), ALU.subtract)
 
-    def keys_a(t0, t1):
-        for B in range(8):
-            tr(R("itT", ALL, B, S(32 * t0, 32 * t1)), R("it", ALL, S(256 * t0 + B, 256 * t1, 8)))
+    def key_consts():
+        act(R("mk"), R("mk"), AF.Identity, bias=col("pf", 0))
+        act(R("pk", ALL, S(0, 256)), R("mk"), AF.Identity, bias=2048.0, scale=8191.0)
+
+    def late_consts():
+        mm(R("pb", ALL, S(0, 128)), R("Z", ALL, S(17, 145)), R("Ib"), True, True)
+        mm(R("pb", ALL, S(128, 256)), R("Z", ALL, S(32, 160)), R("Inb"), True, True)
+        act(R("Bs"), R("pb", ALL, S(0, 256)))
+        fill(col("pb", 255), -BIG)
+        fill(col("pt", 256), BIG)
+        act(R("IK"), R("Iw", ALL, S(16, 144)), scale=-K)
+        act(R("c2"), R("mk"), AF.Identity, bias=-4096.0, scale=-16382.0)
+        act(R("pk", ALL, S(256, 512)), R("mk"), AF.Identity, bias=-2048.0)
+        act(R("In"), R("Iw", ALL, S(16, 144)), scale=-1.0)
+        if "Ha" in " ".join(OPT["plan"]):
+            act(R("mS"), R("mk"), AF.Identity, bias=2048.0)
+
+    def lists(t):
+        c = S(256 * t, 256 * t + 256)
+        cp(R("it16", ALL, c), R("it", ALL, c))
 
     def keys(t):
-        for v in range(2):
-            tt(R("E", ALL, S(256 * t + v, 256 * t + 256, 2)), R("itT", ALL, ALL, S(32 * t + 16 * v, 32 * t + 16 * v + 16)),
-               R("cI", ALL, ALL, S(16 * v, 16 * v + 16)), ALU.add)
         c = S(256 * t, 256 * t + 256)
+        tt(R("Et"), R("it", ALL, c), R("pk", ALL, S(0, 256)), ALU.add)
+        tr(R("E", ALL, c), R("Et"))
         act(R("En", ALL, c), R("E", ALL, c), scale=-1.0)
 
     def hops():
@@ -345,137 +341,134 @@ def rank_program(g, core, T, topo):
             op("v", lambda t=t: g.vector.tensor_reduce(T.nh[:, t:t + 1], T.hm[:, 8 * t:8 * t + 8], AX.X, ALU.add, negate=True),
                [R("nh", ALL, S(t, t + 1))], [R("hm", ALL, S(8 * t, 8 * t + 8))])
 
-    def first_rows():
-        cp(R("HL", ALL, S(0, 256)), R("rs"))
-        tt(R("HL", ALL, S(256, 512)), R("rs"), R("HL", ALL, S(0, 256)), ALU.subtract)
-        dma("s", R("Rw", S(0, 128, 16), ALL), R("HL", ALL, S(0, 256)), False)
-        dma("s", R("Rw", S(1, 128, 16), ALL), R("HL", ALL, S(256, 512)), False)
+    spare = [0, 512, 1024, 1536]
+    begun = {}
 
-    slot = [0]
+    def bank():
+        return spare.pop(0)
 
-    def votes(Sn, a, b, mode):
+    def votes(Sn, a, b, mode, finish=True):
         w = b - a
-        if w > 511:
-            votes(Sn, a, a + w // 2, mode)
-            votes(Sn, a + w // 2, b, mode)
-            return
-        p0 = 512 * (slot[0] % 4)
-        slot[0] += 1
-        if mode in "pqz":
-            pos, neg = (R("Ib"), R("Inb")) if Sn == "spb" else (R("Iw", ALL, S(16, 144)), R("In"))
-            o = R("pv", ALL, S(p0, p0 + w + 1))
-            mm(o, pos, R(Sn, ALL, S(a - 1, b)), True, False)
-            mm(o, neg, R(Sn, ALL, S(a, b + 1)), False, True)
-            act(R("r1", ALL, S(a, b)), R("pv", ALL, S(p0, p0 + w)), AF.Relu, scale=float(2 ** 36))
-            nxt = R("pv", ALL, S(p0 + 1, p0 + w + 1))
-            if mode == "p":
-                tt(R("V", ALL, S(a, b)), nxt, R("r1", ALL, S(a, b)), ALU.subtract)
-            elif mode == "z":
-                act(R("r2", ALL, S(a, b)), nxt, AF.Relu, scale=-float(2 ** 36))
-                p1 = 512 * (slot[0] % 4)
-                slot[0] += 1
-                nxt = R("pv", ALL, S(p1, p1 + w))
-                mm(nxt, R("Inb"), R("r1", ALL, S(a, b)), True, False)
-                mm(nxt, R("Inb"), R("r2", ALL, S(a, b)), False, True)
-                act(R("V", ALL, S(a, b)), nxt)
+        pos, neg = (R("Ib"), R("Inb")) if Sn == "spb" else (R("Iw", ALL, S(16, 144)), R("In"))
+        if a not in begun:
+            p0 = begun[a] = bank()
+            if mode in "pqwz":
+                o = R("pv", ALL, S(p0, p0 + w + 1))
+                mm(o, pos, R(Sn, ALL, S(a - 1, b)), True, False)
+                mm(o, neg, R(Sn, ALL, S(a, b + 1)), False, True)
+            elif mode == "c":
+                mm(R("pv", ALL, S(p0, p0 + w)), pos, R(Sn, ALL, S(a - 1, b - 1)), True, True)
             else:
-                p1 = 512 * (slot[0] % 4)
-                slot[0] += 1
-                nxt = R("pv", ALL, S(p1, p1 + w))
-                mm(nxt, pos, R(Sn, ALL, S(a, b)), True, False)
-                mm(nxt, neg, R(Sn, ALL, S(a + 1, b + 1)), False, False)
-                mm(nxt, R("Inb"), R("r1", ALL, S(a, b)), False, True)
-                act(R("V", ALL, S(a, b)), nxt)
+                act(R("pv", ALL, S(p0, p0 + w)), R(Sn, ALL, S(a - 1, b - 1)))
+        if not finish:
+            return
+        p0 = begun.pop(a)
+        low, nxt = R("pv", ALL, S(p0, p0 + w)), R("pv", ALL, S(p0 + 1, p0 + w + 1))
+        r1, r2, huge = R("r1", ALL, S(p0, p0 + w)), R("r2", ALL, S(p0, p0 + w)), float(2 ** 36)
+        if mode == "w":
+            act(R("r2", ALL, S(p0, p0 + w + 1)), R("pv", ALL, S(p0, p0 + w + 1)))
+            ts(r1, r2, huge, 0.0, ALU.mult, ALU.max)
+            mm(low, R("Ib"), R("r2", ALL, S(p0 + 1, p0 + w + 1)), True, False)
+        elif mode in "pqz":
+            act(r1, low, AF.Relu, scale=huge)
+        if mode == "p":
+            tt(R("V", ALL, S(a, b)), nxt, r1, ALU.subtract)
+        elif mode in "qwz":
+            if mode == "z":
+                act(r2, nxt, AF.Relu, scale=-huge)
+                mm(low, R("Inb"), r2, True, False)
+            if mode == "q":
+                mm(low, pos, R(Sn, ALL, S(a, b)), True, False)
+                mm(low, neg, R(Sn, ALL, S(a + 1, b + 1)), False, False)
+            mm(low, R("Inb"), r1, False, True)
+            act(R("V", ALL, S(a, b)), low)
         else:
-            act(R("pv", ALL, S(p0, p0 + w + 1)), R(Sn, ALL, S(a - 1, b)))
-            tt(R("A", ALL, S(p0, p0 + w)), R("pv", ALL, S(p0, p0 + w)), R(Sn, ALL, S(a + 1, b + 1)), ALU.max)
-            tt(R("V", ALL, S(a, b)), R("pv", ALL, S(p0 + 1, p0 + w + 1)), R("A", ALL, S(p0, p0 + w)), ALU.subtract)
+            tt(low, low, R(Sn, ALL, S(a + 1, b + 1)), ALU.max)
+            tt(R("V", ALL, S(a, b)), R(Sn, ALL, S(a, b)), low, ALU.subtract)
+        spare.append(p0)
 
     def rows_split(t):
-        qf = R("pa", ALL, S(256, 512))
-        cp(R("Qf"), R("Q%d" % t))
-        act(R("HL", ALL, S(0, 256)), R("Qf"))
-        act(qf, R("HL", ALL, S(0, 256)))
-        tt(R("HL", ALL, S(256, 512)), R("Qf"), qf, ALU.subtract)
+        cp(R("Qf"), R("Q%d" % (t - 1)) if t else R("rs"))
+        act(R("HL"), R("Qf"))
 
-    def rows_pe(r):
-        o = R("pv", ALL, S(256 * (r % 8), 256 * (r % 8) + 256))
-        mm(o, R("Ym", ALL, S(144 * r + 1, 144 * r + 129)), R("HL", ALL, S(0, 256)), True, False)
-        mm(o, R("Ym", ALL, S(144 * r, 144 * r + 128)), R("HL", ALL, S(256, 512)), False, True)
+    def rows(t):
+        p0 = held[0]
+        for r in range(16):
+            c = S(r, W, 16) if t else S(256 * r, 256 * r + 256)
+            act(R("Rw", ALL, c), R("pv", ALL, S(p0 + 256 * (r % 2), p0 + 256 * (r % 2) + 256)), scale=col("Pm", r // 2))
+        spare.append(p0)
 
-    def rows_act(r):
-        act(R("Rw", ALL, S(r, W, 16)), R("pv", ALL, S(256 * (r % 8), 256 * (r % 8) + 256)))
+    held = [0]
 
-    K = float(2 ** 27)
+    def row_parts():
+        p0 = held[0] = bank()
+        for v in range(2):
+            o = R("pv", ALL, S(p0 + 256 * v, p0 + 256 * v + 256))
+            mm(o, R("Sw", ALL, v, ALL), R("Qf"), True, False)
+            mm(o, R("Sb", ALL, v, ALL), R("HL"), False, True)
 
     def moved(t):
+        row_parts()
         for j in range(4):
             for B in (2 * j, 2 * j + 1):
-                src = G(R("V"), R("it16", ALL, S(96 * B + 32 * t, 96 * B + 32 * t + 32)))
+                src = G(R("V"), R("it16", ALL, S(256 * t + 32 * B, 256 * t + 32 * B + 32)))
                 out = R("Vg", ALL, S(512 * B, 512 * B + 512))
                 if OPT["ve"][t][B] == "a":
                     act(out, src, AF.Sign, bias=2.0 ** -40)
                 else:
                     ts(out, src, 0.0, -15.0 / 32, ALU.is_ge, ALU.add)
             for r in range(16):
-                mm(R("pa", ALL, S(64 * j, 64 * j + 64)), R("Z2", ALL, S(32 - 2 * r, 160 - 2 * r)),
+                mm(R("pa", ALL, S(64 * j, 64 * j + 64)), R("Z2", ALL, S(32 - r, 160 - r)),
                    R("Vg", ALL, S(1024 * j + r, 1024 * j + 1024, 16)), r == 0, r == 15)
                 if r == 0:
                     for B in (2 * j, 2 * j + 1):
                         if OPT["ve"][t][B] == "a":
                             mm(R("pa", ALL, S(32 * B, 32 * B + 32)), R("Ib"), R("kb"), False, False)
 
-    def rows():
-        for r in range(0, 16, 2):
-            rows_pe(r)
-            rows_pe(r + 1)
-            rows_act(r)
-            rows_act(r + 1)
-
     def back(lo, hi, step=1):
         return S(hi - 1, lo - 1 if lo else None, -step)
 
     def nearest(t):
+        parts = [S(a, b) for a, b in OPT["parts"][t]]
+        tmp = {}
+        for c in parts:
+            p0 = bank()
+            tmp[c.start] = R("pv", ALL, S(p0, p0 + c.stop - c.start))
+            mm(tmp[c.start], R("IK"), R("c2", ALL, c), True, False)
         tr(R("Xc"), R("pa", ALL, S(0, 256)))
-        for v in range(2):
-            e = 256 * t + v
-            scan(R("Wn", ALL, S(v, 256, 2)), R("Xc", ALL, S(v, 256, 2)), R("E", ALL, S(e, e + 255, 2)), -BIG, ALU.max, ALU.min)
-            scan(R("Wn", ALL, back(256 + v, 511 + v, 2)), R("Xc", ALL, back(v, 255 + v, 2)), R("En", ALL, back(e, e + 255, 2)),
-                 -BIG, ALU.max, ALU.min)
-        tr(R("C1"), R("Wn", ALL, S(224, 288)))
-        scan(R("C2", ALL, S(1, 32)), R("C1", ALL, S(0, 31)), R("C1", ALL, S(0, 31)), -BIG, ALU.max, ALU.max)
-        scan(R("C2", ALL, back(32, 63)), R("C1", ALL, back(33, 64)), R("C1", ALL, back(33, 64)), -BIG, ALU.max, ALU.max)
-        tr(R("C3"), R("C2"))
-        for v in range(2):
-            ts(R("W1", ALL, S(8, 16), S(16 * v, 16 * v + 16)), R("Wn", ALL, S(256 + v, 512, 2)), R("C3", ALL, S(32 + v, 33 + v)),
-               -1.0, ALU.max, ALU.mult)
-        for v in range(2):
-            ts(R("W1", ALL, S(0, 8), S(16 * v, 16 * v + 16)), R("Wn", ALL, S(v, 256, 2)), R("C3", ALL, S(30 + v, 31 + v)),
-               None, ALU.max)
-        H = OPT["halves"]
-        nb = 8 // H
-        hs = [(S(32 * nb * h, 32 * nb * (h + 1)), S(256 + 32 * nb * h, 256 + 32 * nb * (h + 1)),
-               R("W1", ALL, S(nb * h, nb * (h + 1)), ALL), R("W1", ALL, S(8 + nb * h, 8 + nb * (h + 1)), ALL)) for h in range(H)]
-        tmp = lambda c: R("pb" if c.start else "pt", ALL, c)
-        for c, c2, L, Rr in hs:
-            tt(tmp(c), R("pk", ALL, c), Rr, ALU.subtract)
-        for c, c2, L, Rr in hs:
-            tt(tmp(c), tmp(c), L, ALU.subtract)
-        for c, c2, L, Rr in hs:
-            ts(tmp(c), tmp(c), -1.0, K, ALU.add, ALU.mult)
-        for c, c2, L, Rr in hs:
-            tt(tmp(c), tmp(c), L, ALU.max)
-        for c, c2, L, Rr in hs:
-            tt(R("ch", ALL, c), tmp(c), Rr, ALU.min)
-        for c, c2, L, Rr in hs:
-            ts(R("ee", ALL, c), R("ch", ALL, c), 8191, None, ALU.bitwise_and)
-        for B in range(8):
-            tr(R("en", ALL, S(B, 256, 8)), R("ee", ALL, S(32 * B, 32 * B + 32)))
-        top, loc = S(160, 256), S(0, 160)
-        tt(R("su", ALL, top), R("pk", ALL, S(416, 512)), R("en", ALL, top), ALU.add)
-        tt(R("su", ALL, loc), R("pk", ALL, S(256, 416)), R("en", ALL, loc), ALU.add)
-        ts(R("s16", ALL, top), R("su", ALL, top), 4095.0, None, ALU.min)
-        ts(R("s16", ALL, loc), R("su", ALL, loc), 4095.0, None, ALU.min)
+        e0 = 256 * t
+        for keys_, j in (("E", 0), ("En", 15)):
+            first = R(keys_, ALL, S(e0 + j, e0 + 256, 16))
+            tt(first, R("Xc", ALL, S(j, 256, 16)), first, ALU.min)
+        scan(R("Wf"), R("Xc"), R("E", ALL, S(e0, e0 + 256)), -BIG, ALU.max, ALU.min)
+        scan(R("Wb", ALL, back(0, 256)), R("Xc", ALL, back(0, 256)), R("En", ALL, back(e0, e0 + 256)), -BIG, ALU.max, ALU.min)
+        tr(R("Lf"), R("Wf"))
+        mm(R("pb", ALL, S(256, 511)), R("Bs", ALL, 0, ALL), R("Lf", ALL, S(0, 255)), True, True)
+        tr(R("Lb"), R("Wb"))
+        mm(R("pt", ALL, S(1, 256)), R("Bs", ALL, 1, ALL), R("Lb", ALL, S(1, 256)), True, True)
+        act(R("Xn"), R("Lb"), scale=-1.0)
+        scan(R("Lk"), R("pb", ALL, S(255, 511)), R("Lf"), -BIG, ALU.max, ALU.max)
+        for c in parts:
+            mm(tmp[c.start], R("IK"), R("Lk", ALL, c), False, False)
+        scan(R("Rk", ALL, back(0, 256)), R("pt", ALL, back(1, 257)), R("Xn", ALL, back(0, 256)), BIG, ALU.min, ALU.min)
+        for c in parts:
+            mm(tmp[c.start], R("IK"), R("Rk", ALL, c), False, True)
+        if t < 2:
+            keys(t + 1)
+            lists(t + 1)
+        for grp in OPT["ilv"][t]:
+            cs = [parts[i] for i in grp]
+            for c in cs:
+                tt(tmp[c.start], tmp[c.start], R("Lk", ALL, c), ALU.max)
+            for c in cs:
+                tt(R("ch", ALL, c), tmp[c.start], R("Rk", ALL, c), ALU.min)
+            for c in cs:
+                ts(R("en", ALL, c), R("ch", ALL, c), 8191, None, ALU.bitwise_and)
+            for c in cs:
+                tt(R("su", ALL, c), R("pk", ALL, S(256 + c.start, 256 + c.stop)), R("en", ALL, c), ALU.add)
+            for c in cs:
+                ts(R("s16", ALL, c), R("su", ALL, c), 4095.0, None, ALU.min)
+                spare.append(tmp[c.start][1][1].start)
 
     dst, pieces, qeng = route(T, topo, rank)
     _d, inpieces, inq = route(T, topo, (rank - 1) % N)
@@ -492,7 +485,7 @@ def rank_program(g, core, T, topo):
                                            src=in_[2], dst=T["L%d" % t][:, a:b]))
         s = "s%d" % (4 * t)
         return op("r", lambda: g.remote_dma_fused(moves, local_sem=T.sem[s]), [], reads, sem=s,
-                  inc=len(pieces[0][3]) + len(pieces[1][3]), cost=0.8, lat=OPT["rlat"][1])
+                  inc=len(pieces[0][3]) + len(pieces[1][3]), cost=0.9, lat=OPT["rlat"][1])
 
     def send(t, i):
         if i < len(pieces):
@@ -507,7 +500,7 @@ def rank_program(g, core, T, topo):
         rid, pid, _s = topo.addr(to)
         s = "s%d" % (4 * t + i)
         return op("r", lambda: g.remote_dma(out[2], in_[2], rs, T.sem[s], pid, rid, bits(eng)), [], [in_], sem=s,
-                  inc=len(eng), cost=0.8, lat=OPT["rlat"][i])
+                  inc=len(eng), cost=0.9, lat=OPT["rlat"][i])
 
     def arrive(t, sent):
         for i, (a, b, relay, eng) in enumerate(inpieces):
@@ -526,8 +519,8 @@ def rank_program(g, core, T, topo):
     def rgath(q, k0, k1):
         gath(q, R("Vg", ALL, S(16 * k0, 16 * k1)), R("Rw"), R("s16", ALL, S(k0, k1)))
 
-    def rpick(t, k0, k1, bank):
-        o = R(bank, ALL, S(k0, k1))
+    def rpick(t, k0, k1, pb):
+        o = R(pb, ALL, S(k0, k1))
         turn = t == 0 and k0 < 160
         z = 16 if turn else 32
         for r in range(16):
@@ -535,12 +528,12 @@ def rank_program(g, core, T, topo):
         if turn:
             mm(o, R("Iw", ALL, S(0, 128)), R("hd", ALL, S(k0, k1)), False, True)
 
-    def qlist(t, k0, k1, bank):
+    def qlist(t, k0, k1, pb):
         c = S(k0, k1)
         if t == 0 and k0 < 160:
-            cp(R("Qx", ALL, c), R(bank, ALL, c))
+            cp(R("Qx", ALL, c), R(pb, ALL, c))
         else:
-            tt(R("Qx", ALL, c), R(bank, ALL, c), R("hd", ALL, c), ALU.add)
+            tt(R("Qx", ALL, c), R(pb, ALL, c), R("hd", ALL, c), ALU.add)
         ts(R("Qi", ALL, c), R("Qx", ALL, c), 4095, None, ALU.bitwise_and)
         if k0 < 160:
             cp(R("Q%d" % t, ALL, S(96 + k0, 96 + k1)), R("Qi", ALL, c))
@@ -554,72 +547,67 @@ def rank_program(g, core, T, topo):
         if t == 0:
             mm(R("pb", ALL, S(0, 160)), R("Iw", ALL, S(0, 128)), R("su", ALL, S(0, 160)), True, True)
             ts(R("s16a"), R("pb", ALL, S(0, 160)), 4095.0, None, ALU.min)
-        sent = []
-        for i, (a, b, _r, _e) in enumerate(pieces):
-            gath(OPT["te"][t][i], R("Ts0" if t == 0 else "Ts", ALL, S(a, b)), R(old, ALL, S(0, W)),
-                 R("s16", ALL, S(160 + a // 16, 160 + b // 16)))
-            if i == 1:
-                sent += [send_two(t)] * 2
-            if i == 2:
-                sent.append(send(t, i))
-        if OPT["hd"] == "v":
-            ts(R("hd"), R("en"), -4096.0, R("nh", ALL, S(t, t + 1)), ALU.add, ALU.mult)
-        else:
-            e = R("pa", ALL, S(256, 512))
-            mm(e, R("Iw", ALL, S(16, 144)), R("su"), True, False)
-            mm(e, R("In"), R("mS"), False, True)
-            nh = R("nh", ALL, S(t, t + 1))
-            op("a", lambda: g.scalar.activation(T.hd[:], e[2], AF.Copy, scale=nh[2]), [R("hd")], [e, nh])
-        for q, k0, k1 in OPT["rt"][t]:
-            rgath(q, k0, k1)
-        rpick(t, 160, 256, "pa")
-        qlist(t, 160, 256, "pa")
-        sent.append(send(t, len(pieces)))
-        arrive(t, sent)
+        sent = {}
 
         def mul(a, b):
             rec = "recb" if (t == 2 and a < X) else "reca"
             other = R("L%d" % t, ALL, S(a, b)) if a < X else R("Tl", ALL, S(a - X, b - X))
             tt(R(new, ALL, S(a, b)), G(R(rec), R("Q%d" % t, ALL, S(a // 16, b // 16))), other, ALU.mult)
 
-        nr, nv, lc = 0, 0, OPT["lc"]
-        for what, q, k0, k1 in OPT["loc"][t]:
-            if what == "R":
-                rgath(q, k0, k1)
-                rpick(t, k0, k1, "pb" if nr % 2 == 0 else "pt")
-                qlist(t, k0, k1, "pb" if nr % 2 == 0 else "pt")
+        nr = 0
+        for step in OPT["plan"][t].split():
+            what, q, arg = step[0], step[1:2], [int(z) for z in step[2:].split("-") if z]
+            if what == "H" and q == "v":
+                ts(R("hd"), R("en"), -4096.0, col("nh", t), ALU.add, ALU.mult)
+            elif what == "H":
+                e = R("pa", ALL, S(256, 512))
+                mm(e, R("In"), R("mS"), True, False)
+                mm(e, R("Iw", ALL, S(16, 144)), R("su"), False, True)
+                act(R("hd"), e, scale=col("nh", t))
+            elif what == "T":
+                i = arg[0]
+                a, b = pieces[i][:2]
+                gath(q, R("Ts0" if t == 0 else "Ts", ALL, S(a, b)), R(old, ALL, S(0, W)),
+                     R("s16", ALL, S(160 + a // 16, 160 + b // 16)))
+                if i == 1:
+                    sent[0] = sent[1] = send_two(t)
+                if i == 2:
+                    sent[2] = send(t, 2)
+            elif what == "R":
+                rgath(q, *arg)
+            elif what == "Q":
+                k0, k1 = arg
+                pb = "pa" if k1 == 256 else "pb" if nr % 2 == 0 else "pt"
                 nr += 1
-                continue
-            gath(q, R("Tl", ALL, S(16 * k0, 16 * k1)), lwin, R("s16a" if t == 0 else "s16", ALL, S(k0, k1)))
-            mul(X + 16 * k0, X + 16 * k1)
-            while t < 2 and nv < len(lc) - 1 and (lc[nv + 1] < X + 16 * k1 - OPT["lag"] or k1 == 160):
-                votes(new, lc[nv], lc[nv + 1], OPT["lmode"][nv])
-                nv += 1
-        if t < 2:
-            rows_split(t)
-        if t == 2:
-            for j in range(3):
-                mm(R("pv", ALL, S(512 * j, 512 * j + 512)), R("Iw", ALL, S(32, 160)),
-                   R(new, ALL, S(2048 + 512 * j, 2560 + 512 * j)), True, j >= OPT["pj"])
-            o = R("pv", ALL, S(X, 2048))
-            mm(o, R("Iw", ALL, S(16, 144)), R(new, ALL, S(X, 2048)), True, False)
-            mm(o, R("Iw", ALL, S(16, 144)), R(new, ALL, S(3584, W)), False, True)
-            act(R("Yo", ALL, S(X, 2048)), o)
-            store("ss", S(X, 2048), rank)
-        for j in range(3):
-            mul(512 * j, 512 * j + 512)
-            if t == 2:
-                c = S(512 * j, 512 * j + 512)
-                if j < OPT["pj"]:
+                rpick(t, k0, k1, pb)
+                qlist(t, k0, k1, pb)
+                if k1 == 256:
+                    sent[3] = send(t, 3)
+            elif what == "L":
+                k0, k1 = 32 * arg[0], 32 * arg[0] + 32
+                gath(q, R("Tl", ALL, S(16 * k0, 16 * k1)), lwin, R("s16a" if t == 0 else "s16", ALL, S(k0, k1)))
+            elif what == "X":
+                arrive(t, [sent[i] for i in range(4)])
+            elif what == "M":
+                mul(*arg)
+            elif what in "DW":
+                votes(new, arg[0], arg[1], q, what == "W")
+            elif what == "S":
+                rows_split(t + 1)
+            elif what == "K":
+                keys(t + 1)
+            elif what == "U":
+                c = S(*arg)
+                z = 32 if c.start < X else 16
+                mm(R("pv", ALL, c), R("Iw", ALL, S(z, z + 128)), R(new, ALL, S(2048 + c.start, 2048 + c.stop)), True, q == "v")
+            else:
+                c = S(*arg)
+                if q == "a":
                     mm(R("pv", ALL, c), R("Iw", ALL, S(16, 144)), R(new, ALL, c), False, True)
                     act(R("Yo", ALL, c), R("pv", ALL, c))
                 else:
                     tt(R("Yo", ALL, c), R("pv", ALL, c), R(new, ALL, c), ALU.add)
-                store("ss" if j < 2 else "sa", c, rank + 1)
-        if t < 2:
-            rc = OPT["rc"]
-            for j in range(len(rc) - 1):
-                votes(new, rc[j], rc[j + 1], OPT["rmode"][j])
+                store("ss", c, rank + 1 if c.start < X else rank)
 
     def store(q2, c, k):
         k %= 8
@@ -628,25 +616,18 @@ def rank_program(g, core, T, topo):
             dma(q2[1], R("y", S(0, 16 * k), c), R("Yo", S(128 - 16 * k, 128), c), False)
 
     cuts = OPT["c0"]
-    lists(0, 1)
-    for i in range(len(cuts) - 1):
-        votes("spb", cuts[i], cuts[i + 1], OPT["m0"][i])
-    first_rows()
-    turned("ss", "recb", ALL, "rec", ALL, rank + 1)
+    named = {"cnt": count_consts, "row": row_consts, "key": key_consts, "late": late_consts, "lists": lambda: lists(0),
+             "hops": hops, "split": lambda: rows_split(0), "moved": lambda: moved(0), "keys": lambda: keys(0)}
+    for step in OPT["pre"].split():
+        if step in named:
+            named[step]()
+        else:
+            votes("spb", cuts[int(step)], cuts[int(step) + 1], OPT["m0"][int(step)])
     for t in range(3):
-        if t == 1:
-            lists(1, 3)
-        moved(t)
-        if t == 0:
-            keys_a(0, 1)
-            late()
-            hops()
-        if t == 1:
-            keys_a(1, 3)
-        keys(t)
+        if t:
+            moved(t)
         nearest(t)
-        if t > 0:
-            rows()
+        rows(t)
         shift(t)
 
     n = len(ops)
@@ -661,43 +642,48 @@ def rank_program(g, core, T, topo):
     lane = lambda i: lanes[i]
     cost = [o["cost"] for o in ops]
 
-    def lay(prio, nxt, prv, ready, slack):
-        left = [len(p) for p in prv]
-        pools = {}
+    def lay(order, prv, ready):
+        busy, start = {}, [0.0] * n
+        for i in order:
+            t = max([ready[i]] + [start[d] + cost[d] + gap for d, gap in prv[i]])
+            if lanes[i] != "x":
+                row = busy.setdefault(lanes[i], [])
+                k = len(row)
+                while k and row[k - 1][0] > t:
+                    k -= 1
+                if k and row[k - 1][1] > t:
+                    t = row[k - 1][1]
+                while k < len(row) and row[k][0] < t + cost[i] + OPT["fit"]:
+                    t = max(t, row[k][1])
+                    k += 1
+                row.insert(k, (t, t + cost[i]))
+            start[i] = t
+        return start
+
+    def greedy():
+        left = [len(p) for p in pred]
+        ready, start, pools, free, done = [0.0] * n, [0.0] * n, {}, {}, 0
         for i in range(n):
             if not left[i]:
                 pools.setdefault(lanes[i], []).append(i)
-        free, out, ends = {}, [], [0.0] * n
-        while len(out) < n:
+        while done < n:
             first, q = min((max(min(ready[i] for i in p), free.get(k, 0.0)), k) for k, p in pools.items() if p)
-            i = max((j for j in pools[q] if ready[j] <= first + (OPT["tslack"] if q == "t" else slack)), key=lambda j: (prio[j], -j))
+            i = min(j for j in pools[q] if ready[j] <= first + OPT["slack"].get(q, 0.0))
             pools[q].remove(i)
-            out.append(i)
-            ends[i] = max(ready[i], free.get(q, 0.0)) + cost[i]
+            done += 1
+            start[i] = max(ready[i], free.get(q, 0.0))
             if q != "x":
-                free[q] = ends[i]
-            for j, gap in nxt[i]:
-                ready[j] = max(ready[j], ends[i] + gap)
+                free[q] = start[i] + cost[i]
+            for j, gap in succ[i]:
+                ready[j] = max(ready[j], start[i] + cost[i] + gap)
                 left[j] -= 1
                 if not left[j]:
                     pools.setdefault(lanes[j], []).append(j)
-        return out, ends
+        return start
 
-    tail = [0.0] * n
-    for i in range(n - 1, -1, -1):
-        tail[i] = cost[i] + max([ops[i]["lat"]] + [tail[j] + gap for j, gap in succ[i]])
-    best = None
-    rng = np.random.default_rng(1)
-    prio = [-float(i) for i in range(n)]
-    for k in range(OPT["tries"]):
-        out, ends = lay(prio, succ, pred, [0.0] * n, OPT["slack"])
-        span = max(ends[i] + ops[i]["lat"] for i in range(n))
-        if best is None or span < best[0]:
-            best = (span, out, ends)
-        base = ends if k % 4 != 3 else best[2]
-        noise = rng.random(n) * OPT["noise"] * (k % 4 == 3)
-        _o, prio = lay([float(e + z) for e, z in zip(base, noise)], pred, succ, [o["lat"] for o in ops], OPT["slack"])
-    seq = best[1]
+    start = greedy() if OPT["greedy"] else lay(range(n), pred, [0.0] * n)
+    best = (max(start[i] + cost[i] + ops[i]["lat"] for i in range(n)), start)
+    seq = sorted(range(n), key=lambda i: (best[1][i], i))
     SPAN[rank] = best[0]
     place = {i: k for k, i in enumerate(seq)}
     need = set()

@@ -6,15 +6,15 @@ W, X, LOC = 4096, 1536, 2560
 F32, BF, I32, U16 = "float32", "bfloat16", "int32", "uint16"
 SCRATCH = {
     "spa": ("sbuf", [128, W], BF), "spb": ("sbuf", [128, W + 16], BF),
-    "reca": ("sbuf", [128, W], BF), "recb": ("sbuf", [128, W], BF),
+    "reca": ("sbuf", [128, 2 * W + 16], BF), "recb": ("sbuf", [128, 2 * W + 16], BF),
     "Sx": ("sbuf", [128, W + 8], F32), "Sy": ("sbuf", [128, W + 8], F32),
     "Tl": ("sbuf", [128, LOC], F32), "Ts": ("sbuf", [128, X], F32), "Ts0": ("sbuf", [128, X], BF),
     "L0": ("sbuf", [128, X], BF), "L1": ("sbuf", [128, X], F32), "L2": ("sbuf", [128, X], F32),
     "V": ("sbuf", [128, W], BF), "Vg": ("sbuf", [128, W], BF), "Rw": ("sbuf", [128, W], BF),
-    "mS": ("sbuf", [128, 256], F32), "r1": ("sbuf", [128, 2048], BF), "r2": ("sbuf", [128, 2048], BF),
+    "mS": ("sbuf", [128, 256], F32), "r1": ("sbuf", [128, 3584], BF), "r2": ("sbuf", [128, 3584], BF),
     "Yo": ("sbuf", [128, 2048], F32),
     "Q0": ("sbuf", [128, 256], U16), "Q1": ("sbuf", [128, 256], U16), "Q2": ("sbuf", [128, 256], U16),
-    "Qs": ("sbuf", [128, 288], U16), "Qi": ("sbuf", [128, 256], I32), "Qx": ("sbuf", [128, 256], I32),
+    "Qs": ("sbuf", [128, 288], U16), "hy": ("sbuf", [128, 256], F32), "kc": ("sbuf", [128, 160], BF),
     "Qf": ("sbuf", [128, 256], F32), "HL": ("sbuf", [128, 256], BF),
     "it": ("sbuf", [128, 768], I32), "it16": ("sbuf", [128, 768], U16),
     "E": ("sbuf", [128, 768], F32), "En": ("sbuf", [128, 768], F32), "Z2": ("sbuf", [128, 160], BF),
@@ -32,43 +32,48 @@ SCRATCH = {
     "i4": ("sbuf", [128, 8], I32),
     "pc": ("sbuf", [128, 4], I32), "pm": ("sbuf", [128, 8], I32), "pf": ("sbuf", [128, 8], F32),
     "kb": ("sbuf", [128, 32], BF), "mk": ("sbuf", [128, 256], F32),
-    "Iw": ("sbuf", [128, 160], F32), "In": ("sbuf", [128, 128], F32), "Ib": ("sbuf", [128, 128], BF),
+    "Iw": ("sbuf", [128, 160], F32), "In": ("sbuf", [128, 160], F32), "Ib": ("sbuf", [128, 128], BF),
     "Inb": ("sbuf", [128, 128], BF), "Z": ("sbuf", [128, 160], BF),
     "Sw": ("sbuf", [128, 2, 128], F32), "Sb": ("sbuf", [128, 2, 128], BF), "Pm": ("sbuf", [128, 8], F32),
     "pv": ("psum", [128, 2048], F32), "pa": ("psum", [128, 512], F32), "pb": ("psum", [128, 512], F32),
     "pk": ("psum", [128, 512], F32), "pt": ("psum", [128, 512], F32),
 }
 NDMA = 48
-SEMAPHORES = ["v", "a", "t", "p", "sent"] + ["d%d" % i for i in range(NDMA)] + ["s%d" % i for i in range(12)] + \
-    ["r%d" % i for i in range(12)] + ["h%d" % i for i in range(6)]
+SEMAPHORES = ["v", "a", "t", "p", "sent"] + ["d%d" % i for i in range(NDMA)] + ["s%d" % i for i in range(18)] + \
+    ["r%d" % i for i in range(18)] + ["h%d" % i for i in range(6)]
 ROWED = ("spa", "spb", "reca", "recb", "it", "rs", "hrow", "y")
 BIG = float(2 ** 26)
 K = float(2 ** 27)
+ROUND = 1.5 * 2 ** 35
 SPAN = {}
 CELLS = {}
-P01 = ("Rv160-224 Ha Rv224-256 Ta0 Ta1 Ta2 Ra0-64 Q-160-256 X M-1024-1536 Lv0 Rv64-96 Q-0-64 M-1536-2048 Lv2 Ra96-160 La1 La3 "
-       "M-512-1024 M-2048-2560 La4 Q-64-96 Q-96-160 M-3072-3584 M-0-512 M-3584-4096 M-2560-3072 Dz1537-2047 Da2047-2558 "
-       "Da3580-3840 Dz2558-3069 Wz1537-2047 Wa2047-2558 Wz2558-3069 Wa3580-3840 Da511-1022 Dz3840-4096 Wz3840-4096 Da1-511 "
-       "Dz1280-1537 Da3069-3580 Wa511-1022 S Dp1022-1280 Wz1280-1537 Wa1-511 Wa3069-3580 Wp1022-1280")
-P2 = ("Ta0 Ta1 Rv160-256 Ha Ra96-160 Ra32-64 Tv2 Rv64-96 Ra0-32 La0 Q-160-256 Q-0-96 La3 Q-96-160 La4 X La2 La1 M-2560-3072 "
-      "M-0-512 Uv512-1024 M-1280-1536 M-1536-2048 M-3584-4096 M-2048-2560 Uv1536-2048 M-3072-3584 Uv1024-1536 Ua0-512 "
-      "M-512-1024 M-1024-1280 Yv512-1024 Yv1536-2048 Ya0-512 Yv1280-1536 Yv1024-1280")
-OPT = {"greedy": True, "slack": {"v": 0.1, "a": 0.1, "t": 0.1}, "fit": 0.0, "relay": True,
+P0 = ("Rv0-32 La1 Ta0 Hv Q-0-32 Ta1 Rv64-96 Tv2 Ta3 Ra160-256 Ra96-160 Rv32-64 La2 Q-96-160 Q-32-96 Lv0 Tv4 La4 La3 "
+      "M-3072-3584 M-2560-3072 Q-160-256 M-1536-2048 M-2048-2560 X M-3584-4096 Dz2047-2558 M-0-512 Da3840-4096 Da3069-3580 "
+      "Wa3069-3580 M-512-960 Da1537-2047 Wa3840-4096 Dz2558-3069 Dp3580-3840 Wz2558-3069 M-960-1536 Dz1280-1537 Wz2047-2558 "
+      "Wz1280-1537 S Da1-511 Da1022-1280 Wa1-511 Wp3580-3840 Da511-1022 Wa1022-1280 Wa1537-2047 Wa511-1022")
+P1 = ("Ta0 Rv0-64 Ta1 Hv Tv2 Ta3 Ra160-256 La1 Ra96-160 La2 Rv64-96 Q-32-96 Lv0 Q-0-32 Tv4 Q-160-256 Q-96-160 M-2048-2560 "
+      "La3 La4 M-3584-4096 X M-3072-3584 M-2560-3072 M-1536-2048 M-0-512 M-512-960 Da3840-4096 Da1537-2047 M-960-1248 "
+      "Da3069-3580 Wa3840-4096 M-1248-1536 Dz2047-2558 De3580-3840 Dw1-511 Wa3069-3580 Wa1537-2047 Wz2047-2558 Dp2558-3069 "
+      "Da959-1247 Wa959-1247 Da1247-1537 Da511-959 S Wa1247-1537 We3580-3840 Wa511-959 Ww1-511 Wp2558-3069")
+P2 = ("Ta0 Tv1 La4 Rv160-256 Ta2 Ta3 Ha Q-160-256 Rv64-160 Ra0-64 La1 Ta4 La3 Q-0-64 M-2048-2560 Q-96-160 M-3584-4096 X "
+      "M-0-512 M-3072-3584 Uv1024-1536 Q-64-96 M-960-1280 Yv1024-1280 La0 Uv1536-2048 La2 M-2560-3072 Ua0-512 M-512-960 "
+      "M-1280-1536 Uv512-1024 M-1536-2048 Yv512-1024 Yv1536-2048 Yv1280-1536 Ya0-512")
+OPT = {"greedy": True, "slack": {"v": 0.1, "a": 0.1, "t": 0.1}, "fit": 0.0, "relay": (1, 2),
        "parts": [[(160, 256), (0, 160)]] * 3, "ilv": [[(0,), (1,)]] * 3,
-       "pe": 0.46e-3, "cy": 0.86e-3, "fix": 0.025, "gat": 1.45, "dbw": 500e3, "wake": 0.19,
-       "rlat": (4.0, 5.5, 6.5, 4.5), "m0": "pcppppppq",
-       "sp": [0, 1024, 2560, 4096],
+       "pe": 0.49e-3, "cy": 0.84e-3, "fix": 0.025, "gat": 1.35, "dbw": 500e3, "wake": 0.2,
+       "rlat": (0.0, 3.3, 0.0, 3.8, 4.6, 4.2), "rw": 288, "hop": (0.0, 5.7, 3.6), "m0": "pcpppppqp",
+       "sp": [0, 528, 1536, 2816, 4096],
        "c0": [1, 512, 1023, 1534, 2045, 2556, 3067, 3578, 3840, 4096],
-       "ve": ["vavaavav", "avavavav", "avavavav"], "plan": [P01, P01, P2],
-       "pre": "1 cnt 0 row split 3 4 5 key lists 6 2 8 7 moved keys hops late"}
+       "ve": ["avvaavav", "avavavav", "avavavav"], "plan": [P0, P1, P2],
+       "pre": "row 0 1 2 lists 4 cnt 5 6 key 3 hops 7 8 moved split late keys"}
 
 
-def route(T, topo, rank):
+def route(T, topo, rank, t):
     src = T.cores[rank]
     dst = T.cores[(rank + 1) % len(T.cores)]
     eng = topo.engines(src, dst)
     relay = None
-    if topo.chip(src) != topo.chip(dst) and OPT["relay"]:
+    if topo.chip(src) != topo.chip(dst) and t in OPT["relay"]:
         for c in topo.cores_of(src):
             if T.rank_of(c) is None and topo.die(c) != topo.die(src) and topo.may_write(c, dst):
                 relay = c
@@ -78,7 +83,9 @@ def route(T, topo, rank):
     else:
         first, second = eng[len(eng) // 2:], eng[:len(eng) // 2]
     whole = second if relay is not None or topo.chip(src) == topo.chip(dst) else eng
-    return dst, [(1024, X, relay, first), (0, 512, None, second), (512, 1024, None, whole)], whole
+    w = OPT["rw"]
+    return dst, [(X - 2 * w, X - w, relay, first), (0, w, None, second), (X - w, X, relay, first), (w, 2 * w, None, second),
+                 (2 * w, X - 2 * w, None, whole)], whole
 
 
 def bits(engines):
@@ -87,17 +94,18 @@ def bits(engines):
 
 def relay_program(g, core, T, topo):
     for rank in range(len(T.cores)):
-        dst, pieces, _e = route(T, topo, rank)
-        for i, (a, b, relay, eng) in enumerate(pieces):
-            if relay != core:
-                continue
-            rid, pid, _s = topo.addr(dst)
-            on = topo.engines(core, dst)
-            for t in range(3):
-                buf = T["L%d" % t]
-                g.wait_ge(T.sem["h%d" % t], len(eng))
-                g.remote_dma(buf[:, a:b], buf[:, a:b], T.sem["r%d" % (4 * t + i)], T.sem["sent"], pid, rid, bits(on))
-            g.wait_ge(T.sem["sent"], 3 * len(on))
+        dst, pieces, _e = route(T, topo, rank, 2)
+        if pieces[0][2] != core:
+            continue
+        rid, pid, _s = topo.addr(dst)
+        on = topo.engines(core, dst)
+        for t in OPT["relay"]:
+            buf = T["L%d" % t]
+            for i in (0, 2):
+                a, b, _r, eng = pieces[i]
+                g.wait_ge(T.sem["h%d" % (2 * t + i // 2)], len(eng))
+                g.remote_dma(buf[:, a:b], buf[:, a:b], T.sem["r%d" % (6 * t + i)], T.sem["sent"], pid, rid, bits(on))
+        g.wait_ge(T.sem["sent"], 2 * len(OPT["relay"]) * len(on))
 
 
 def rank_program(g, core, T, topo):
@@ -188,7 +196,7 @@ def rank_program(g, core, T, topo):
         deps.discard(me)
         if cost is None:
             cost = price(q, writes, reads)
-        if q in "spr":
+        if q in "spr" and not (writes and writes[0][0] == "y"):
             k = "p" if q == "r" else q
             if k in chain:
                 (deps if q == "p" else order).add(chain[k])
@@ -260,17 +268,18 @@ def rank_program(g, core, T, topo):
             dma(q2[1], R(buf, S(128 - 16 * k, 128), *cols), (src, None, T[src][0:unit * k, scols]))
 
     sp = OPT["sp"]
-    turned("ss", "spb", (S(sp[0], sp[1]),), "sp", S(sp[0], sp[1]), rank + 1)
+    turned("sa", "spb", (S(sp[0], sp[1]),), "sp", S(sp[0], sp[1]), rank + 1)
     for i in range(1, len(sp) - 1):
-        turned("ss", "spb", (S(sp[i], sp[i + 1]),), "sp", S(sp[i], sp[i + 1]), rank + 1)
+        turned("sa", "spb", (S(sp[i], sp[i + 1]),), "sp", S(sp[i], sp[i + 1]), rank + 1)
     turned("ss", "it", (S(0, 256),), "itg", S(0, 256), rank + 1)
     turned("ss", "rs", (ALL,), "rot", ALL, rank + 1, unit=1)
     turned("ss", "it", (S(256, 768),), "itg", S(256, 768), rank)
     dma("s", R("hrow", S(0, 1), S(0, 3 * (8 - rank))), ("hop", None, T.hop[rank:8, :]))
     dma("s", R("hrow", S(0, 1), S(3 * (8 - rank), 27)), ("hop", None, T.hop[0:rank + 1, :]))
     turned("ss", "spa", (ALL,), "sp", ALL, rank)
-    turned("ss", "reca", (ALL,), "rec", ALL, rank)
-    turned("ss", "recb", (ALL,), "rec", ALL, rank + 1)
+    for buf, k in (("reca", rank), ("recb", rank + 1)):
+        for a, b, c in ((0, 2048, 2048), (2048, 6144, 0), (6144, 2 * W + 16, 0)):
+            turned("ss", buf, (S(a, b),), "rec", S(c, c + b - a), k)
 
     iota(R("i1"), [[1, 160]], 112, -1)
     iota(R("pc"), [[0, 4]], 0, 1)
@@ -314,14 +323,13 @@ def rank_program(g, core, T, topo):
         mm(R("pb", ALL, S(0, 128)), R("Z", ALL, S(17, 145)), R("Ib"), True, True)
         mm(R("pb", ALL, S(128, 256)), R("Z", ALL, S(32, 160)), R("Inb"), True, True)
         act(R("Bs"), R("pb", ALL, S(0, 256)))
-        fill(col("pb", 255), -BIG)
-        fill(col("pt", 256), BIG)
         act(R("IK"), R("Iw", ALL, S(16, 144)), scale=-K)
         act(R("c2"), R("mk"), AF.Identity, bias=-4096.0, scale=-16382.0)
         act(R("pk", ALL, S(256, 512)), R("mk"), AF.Identity, bias=-2048.0)
-        act(R("In"), R("Iw", ALL, S(16, 144)), scale=-1.0)
+        act(R("In"), R("Iw"), scale=-1.0)
         if "Ha" in " ".join(OPT["plan"]):
             act(R("mS"), R("mk"), AF.Identity, bias=2048.0)
+            fill(R("kc"), ROUND)
 
     def lists(t):
         c = S(256 * t, 256 * t + 256)
@@ -347,34 +355,46 @@ def rank_program(g, core, T, topo):
     def bank():
         return spare.pop(0)
 
+    def PB(p0, a, b):
+        if p0 < 2048:
+            return R("pv", ALL, S(p0 + a, p0 + b))
+        return R(("pa", "pb", "pt")[p0 // 512 - 4], ALL, S(a, b))
+
     def votes(Sn, a, b, mode, finish=True):
         w = b - a
-        pos, neg = (R("Ib"), R("Inb")) if Sn == "spb" else (R("Iw", ALL, S(16, 144)), R("In"))
+        pos, neg = (R("Ib"), R("Inb")) if Sn == "spb" else (R("Iw", ALL, S(16, 144)), R("In", ALL, S(16, 144)))
         if a not in begun:
             p0 = begun[a] = bank()
             if mode in "pqwz":
-                o = R("pv", ALL, S(p0, p0 + w + 1))
+                o = PB(p0, 0, w + 1)
                 mm(o, pos, R(Sn, ALL, S(a - 1, b)), True, False)
                 mm(o, neg, R(Sn, ALL, S(a, b + 1)), False, True)
+            elif mode in "eg":
+                o = PB(p0, 0, w + 1)
+                if mode == "g":
+                    mm(o, pos, R(Sn, ALL, S(a - 1, b)), True, True)
+                else:
+                    act(o, R(Sn, ALL, S(a - 1, b)))
+                tt(o, o, R(Sn, ALL, S(a, b + 1)), ALU.subtract)
             elif mode == "c":
-                mm(R("pv", ALL, S(p0, p0 + w)), pos, R(Sn, ALL, S(a - 1, b - 1)), True, True)
+                mm(PB(p0, 0, w), pos, R(Sn, ALL, S(a - 1, b - 1)), True, True)
             else:
-                act(R("pv", ALL, S(p0, p0 + w)), R(Sn, ALL, S(a - 1, b - 1)))
+                act(PB(p0, 0, w), R(Sn, ALL, S(a - 1, b - 1)))
         if not finish:
             return
         p0 = begun.pop(a)
-        low, nxt = R("pv", ALL, S(p0, p0 + w)), R("pv", ALL, S(p0 + 1, p0 + w + 1))
+        low, nxt = PB(p0, 0, w), PB(p0, 1, min(w + 1, 512))
         r1, r2, huge = R("r1", ALL, S(p0, p0 + w)), R("r2", ALL, S(p0, p0 + w)), float(2 ** 36)
         if mode == "w":
-            act(R("r2", ALL, S(p0, p0 + w + 1)), R("pv", ALL, S(p0, p0 + w + 1)))
+            act(R("r2", ALL, S(p0, p0 + w + 1)), PB(p0, 0, w + 1))
             ts(r1, r2, huge, 0.0, ALU.mult, ALU.max)
             mm(low, R("Ib"), R("r2", ALL, S(p0 + 1, p0 + w + 1)), True, False)
-        elif mode in "pqz":
+        elif mode in "pqzeg":
             act(r1, low, AF.Relu, scale=huge)
         if mode == "p":
             tt(R("V", ALL, S(a, b)), nxt, r1, ALU.subtract)
-        elif mode in "qwz":
-            if mode == "z":
+        elif mode in "qwzeg":
+            if mode in "zeg":
                 act(r2, nxt, AF.Relu, scale=-huge)
                 mm(low, R("Inb"), r2, True, False)
             if mode == "q":
@@ -388,8 +408,19 @@ def rank_program(g, core, T, topo):
         spare.append(p0)
 
     def rows_split(t):
-        cp(R("Qf"), R("Q%d" % (t - 1)) if t else R("rs"))
-        act(R("HL"), R("Qf"))
+        if t == 0:
+            ts(R("Qf"), R("rs"), 2048.0, None, ALU.add)
+            act(R("HL"), R("Qf"))
+            return
+        p0 = bank()
+        spare.append(p0)
+        o = PB(p0, 0, 256)
+        cp(R("Et"), R("Q%d" % (t - 1)))
+        ts(R("HL"), R("Q%d" % (t - 1)), ROUND, -ROUND, ALU.add, ALU.add)
+        mm(o, R("Iw", ALL, S(16, 144)), R("Et"), True, False)
+        mm(o, R("Inb"), R("HL"), False, True)
+        act(R("Qf"), o, AF.Identity, bias=4096.0)
+        act(R("HL"), o, AF.Identity, bias=4096.0)
 
     def rows(t):
         p0 = held[0]
@@ -408,7 +439,9 @@ def rank_program(g, core, T, topo):
             mm(o, R("Sb", ALL, v, ALL), R("HL"), False, True)
 
     def moved(t):
-        row_parts()
+        spare[:] = [p0 for p0 in spare if p0 < 2048]
+        if t:
+            row_parts()
         for j in range(4):
             for B in (2 * j, 2 * j + 1):
                 src = G(R("V"), R("it16", ALL, S(256 * t + 32 * B, 256 * t + 32 * B + 32)))
@@ -435,6 +468,8 @@ def rank_program(g, core, T, topo):
             p0 = bank()
             tmp[c.start] = R("pv", ALL, S(p0, p0 + c.stop - c.start))
             mm(tmp[c.start], R("IK"), R("c2", ALL, c), True, False)
+        mm(col("pb", 255), R("Inb"), col("kb", 0), True, True)
+        mm(col("pt", 256), R("Ib"), col("kb", 0), True, True)
         tr(R("Xc"), R("pa", ALL, S(0, 256)))
         e0 = 256 * t
         for keys_, j in (("E", 0), ("En", 15)):
@@ -445,17 +480,22 @@ def rank_program(g, core, T, topo):
         tr(R("Lf"), R("Wf"))
         mm(R("pb", ALL, S(256, 511)), R("Bs", ALL, 0, ALL), R("Lf", ALL, S(0, 255)), True, True)
         tr(R("Lb"), R("Wb"))
+        gaps = [len(ops) - 1]
         mm(R("pt", ALL, S(1, 256)), R("Bs", ALL, 1, ALL), R("Lb", ALL, S(1, 256)), True, True)
         act(R("Xn"), R("Lb"), scale=-1.0)
         scan(R("Lk"), R("pb", ALL, S(255, 511)), R("Lf"), -BIG, ALU.max, ALU.max)
         for c in parts:
             mm(tmp[c.start], R("IK"), R("Lk", ALL, c), False, False)
         scan(R("Rk", ALL, back(0, 256)), R("pt", ALL, back(1, 257)), R("Xn", ALL, back(0, 256)), BIG, ALU.min, ALU.min)
+        gaps.append(len(ops) - 1)
         for c in parts:
             mm(tmp[c.start], R("IK"), R("Rk", ALL, c), False, True)
         if t < 2:
+            first = len(ops)
             keys(t + 1)
             lists(t + 1)
+            for i, d in zip(range(first, len(ops)), (gaps[0], gaps[1], gaps[1], gaps[0])):
+                ops[i]["order"].add(d)
         for grp in OPT["ilv"][t]:
             cs = [parts[i] for i in grp]
             for c in cs:
@@ -470,44 +510,42 @@ def rank_program(g, core, T, topo):
                 ts(R("s16", ALL, c), R("su", ALL, c), 4095.0, None, ALU.min)
                 spare.append(tmp[c.start][1][1].start)
 
-    dst, pieces, qeng = route(T, topo, rank)
-    _d, inpieces, inq = route(T, topo, (rank - 1) % N)
-
-    def send_two(t):
+    def send_two(t, i0):
+        dst, pieces, _e = route(T, topo, rank, t)
         moves, reads = [], []
-        for i in (0, 1):
+        for i in (i0, i0 + 1):
             a, b, relay, eng = pieces[i]
             rid, pid, _s = topo.addr(dst if relay is None else relay)
             in_ = R("Ts0" if t == 0 else "Ts", ALL, S(a, b))
             reads.append(in_)
             moves.append(RemoteDMATransfer(dst_ids=[DstId(rid=rid, pnc=pid)], dma_engine_mask=bits(eng),
-                                           remote_sem=T.sem["r%d" % (4 * t + i)] if relay is None else T.sem["h%d" % t],
+                                           remote_sem=T.sem["r%d" % (6 * t + i) if relay is None else "h%d" % (2 * t + i // 2)],
                                            src=in_[2], dst=T["L%d" % t][:, a:b]))
-        s = "s%d" % (4 * t)
+        s = "s%d" % (6 * t + i0)
         return op("r", lambda: g.remote_dma_fused(moves, local_sem=T.sem[s]), [], reads, sem=s,
-                  inc=len(pieces[0][3]) + len(pieces[1][3]), cost=0.9, lat=OPT["rlat"][1])
+                  inc=len(pieces[0][3]) + len(pieces[1][3]), cost=0.9, lat=OPT["rlat"][i0 + 1])
 
     def send(t, i):
+        dst, pieces, qeng = route(T, topo, rank, t)
         if i < len(pieces):
-            a, b, relay, eng = pieces[i]
-            to = dst if relay is None else relay
+            a, b, _r, eng = pieces[i]
             out, in_ = R("L%d" % t, ALL, S(a, b)), R("Ts0" if t == 0 else "Ts", ALL, S(a, b))
-            rs = T.sem["r%d" % (4 * t + i)] if relay is None else T.sem["h%d" % t]
         else:
-            to, eng = dst, qeng
+            eng = qeng
             out, in_ = R("Q%d" % t, ALL, S(0, 96)), R("Qs", ALL, S(96 * t, 96 * t + 96))
-            rs = T.sem["r%d" % (4 * t + i)]
-        rid, pid, _s = topo.addr(to)
-        s = "s%d" % (4 * t + i)
+        rs = T.sem["r%d" % (6 * t + i)]
+        rid, pid, _s = topo.addr(dst)
+        s = "s%d" % (6 * t + i)
         return op("r", lambda: g.remote_dma(out[2], in_[2], rs, T.sem[s], pid, rid, bits(eng)), [], [in_], sem=s,
                   inc=len(eng), cost=0.9, lat=OPT["rlat"][i])
 
     def arrive(t, sent):
+        _d, inpieces, inq = route(T, topo, (rank - 1) % N, t)
         for i, (a, b, relay, eng) in enumerate(inpieces):
             n = len(eng) if relay is None else len(topo.engines(relay, core))
-            op("x", None, [R("L%d" % t, ALL, S(a, b))], [], sem="r%d" % (4 * t + i), inc=n,
-               cost=OPT["rlat"][0] if i == 0 else 0.0, after=[sent[i]])
-        op("x", None, [R("Q%d" % t, ALL, S(0, 96))], [], sem="r%d" % (4 * t + len(inpieces)), inc=len(inq), cost=0.0,
+            op("x", None, [R("L%d" % t, ALL, S(a, b))], [], sem="r%d" % (6 * t + i), inc=n,
+               cost=OPT["hop"][t] if i in (0, 2) else 0.0, after=[sent[i]])
+        op("x", None, [R("Q%d" % t, ALL, S(0, 96))], [], sem="r%d" % (6 * t + len(inpieces)), inc=len(inq), cost=0.0,
            after=[sent[-1]])
 
     def gath(q, out, win, off):
@@ -519,26 +557,21 @@ def rank_program(g, core, T, topo):
     def rgath(q, k0, k1):
         gath(q, R("Vg", ALL, S(16 * k0, 16 * k1)), R("Rw"), R("s16", ALL, S(k0, k1)))
 
-    def rpick(t, k0, k1, pb):
+    def rpick(t, k0, k1, pb, by_scalar):
         o = R(pb, ALL, S(k0, k1))
-        turn = t == 0 and k0 < 160
-        z = 16 if turn else 32
+        z = 0 if t == 0 and k0 < 160 else 16
+        mm(o, R("In", ALL, S(z, z + 128)), R("hy", ALL, S(k0, k1)), True, False)
+        if by_scalar:
+            mm(o, R("Ib"), R("kc", ALL, S(0, k1 - k0)), False, False)
+        mm(o, R("Iw", ALL, S(z, z + 128)), R("hd", ALL, S(k0, k1)), False, False)
         for r in range(16):
-            mm(o, R("Z", ALL, S(z - r, z + 128 - r)), R("Vg", ALL, S(16 * k0 + r, 16 * k1, 16)), r == 0, r == 15 and not turn)
-        if turn:
-            mm(o, R("Iw", ALL, S(0, 128)), R("hd", ALL, S(k0, k1)), False, True)
+            mm(o, R("Z", ALL, S(z + 16 - r, z + 144 - r)), R("Vg", ALL, S(16 * k0 + r, 16 * k1, 16)), False, r == 15)
 
     def qlist(t, k0, k1, pb):
-        c = S(k0, k1)
-        if t == 0 and k0 < 160:
-            cp(R("Qx", ALL, c), R(pb, ALL, c))
-        else:
-            tt(R("Qx", ALL, c), R(pb, ALL, c), R("hd", ALL, c), ALU.add)
-        ts(R("Qi", ALL, c), R("Qx", ALL, c), 4095, None, ALU.bitwise_and)
         if k0 < 160:
-            cp(R("Q%d" % t, ALL, S(96 + k0, 96 + k1)), R("Qi", ALL, c))
+            cp(R("Q%d" % t, ALL, S(96 + k0, 96 + k1)), R(pb, ALL, S(k0, k1)))
         else:
-            cp(R("Qs", ALL, S(96 * t + k0 - 160, 96 * t + k1 - 160)), R("Qi", ALL, c))
+            cp(R("Qs", ALL, S(96 * t + k0 - 160, 96 * t + k1 - 160)), R(pb, ALL, S(k0, k1)))
 
     def shift(t):
         old = ("spb", "Sx", "Sy")[t]
@@ -559,35 +592,39 @@ def rank_program(g, core, T, topo):
             what, q, arg = step[0], step[1:2], [int(z) for z in step[2:].split("-") if z]
             if what == "H" and q == "v":
                 ts(R("hd"), R("en"), -4096.0, col("nh", t), ALU.add, ALU.mult)
+                ts(R("hy"), R("hd"), ROUND, -ROUND, ALU.add, ALU.add)
             elif what == "H":
                 e = R("pa", ALL, S(256, 512))
-                mm(e, R("In"), R("mS"), True, False)
+                mm(e, R("In", ALL, S(16, 144)), R("mS"), True, False)
                 mm(e, R("Iw", ALL, S(16, 144)), R("su"), False, True)
+                act(R("hy"), e, AF.Identity, bias=ROUND, scale=col("nh", t))
                 act(R("hd"), e, scale=col("nh", t))
             elif what == "T":
                 i = arg[0]
-                a, b = pieces[i][:2]
+                a, b = route(T, topo, rank, t)[1][i][:2]
                 gath(q, R("Ts0" if t == 0 else "Ts", ALL, S(a, b)), R(old, ALL, S(0, W)),
                      R("s16", ALL, S(160 + a // 16, 160 + b // 16)))
-                if i == 1:
-                    sent[0] = sent[1] = send_two(t)
-                if i == 2:
-                    sent[2] = send(t, 2)
+                if i in (1, 3):
+                    sent[i - 1] = sent[i] = send_two(t, i - 1)
+                if i == 4:
+                    sent[i] = send(t, i)
             elif what == "R":
                 rgath(q, *arg)
             elif what == "Q":
                 k0, k1 = arg
                 pb = "pa" if k1 == 256 else "pb" if nr % 2 == 0 else "pt"
                 nr += 1
-                rpick(t, k0, k1, pb)
+                rpick(t, k0, k1, pb, "Ha" in OPT["plan"][t])
                 qlist(t, k0, k1, pb)
                 if k1 == 256:
-                    sent[3] = send(t, 3)
+                    sent[5] = send(t, 5)
+                if nr == OPT["plan"][t].count("Q"):
+                    spare.extend((2048, 2560, 3072))
             elif what == "L":
                 k0, k1 = 32 * arg[0], 32 * arg[0] + 32
                 gath(q, R("Tl", ALL, S(16 * k0, 16 * k1)), lwin, R("s16a" if t == 0 else "s16", ALL, S(k0, k1)))
             elif what == "X":
-                arrive(t, [sent[i] for i in range(4)])
+                arrive(t, [sent[i] for i in range(6)])
             elif what == "M":
                 mul(*arg)
             elif what in "DW":
@@ -607,7 +644,7 @@ def rank_program(g, core, T, topo):
                     act(R("Yo", ALL, c), R("pv", ALL, c))
                 else:
                     tt(R("Yo", ALL, c), R("pv", ALL, c), R(new, ALL, c), ALU.add)
-                store("ss", c, rank + 1 if c.start < X else rank)
+                store("sa", c, rank + 1 if c.start < X else rank)
 
     def store(q2, c, k):
         k %= 8
@@ -617,7 +654,7 @@ def rank_program(g, core, T, topo):
 
     cuts = OPT["c0"]
     named = {"cnt": count_consts, "row": row_consts, "key": key_consts, "late": late_consts, "lists": lambda: lists(0),
-             "hops": hops, "split": lambda: rows_split(0), "moved": lambda: moved(0), "keys": lambda: keys(0)}
+             "hops": hops, "split": lambda: (rows_split(0), row_parts()), "moved": lambda: moved(0), "keys": lambda: keys(0)}
     for step in OPT["pre"].split():
         if step in named:
             named[step]()

import numpy as np
from concourse.bass import DstId, RemoteDMATransfer
from concourse.mybir import AluOpType as ALU, AxisListType as AX, ActivationFunctionType as AF

W, X, LOC = 4096, 1536, 2560
F32, BF, I32, U16 = "float32", "bfloat16", "int32", "uint16"
SCRATCH = {
    "spa": ("sbuf", [128, W], BF), "spb": ("sbuf", [128, W + 16], BF),
    "reca": ("sbuf", [128, 2 * W + 16], BF), "recb": ("sbuf", [128, 2 * W + 16], BF),
    "Sx": ("sbuf", [128, W + 8], F32), "Sy": ("sbuf", [128, W + 8], F32),
    "Tl": ("sbuf", [128, LOC], F32), "Ts": ("sbuf", [128, X], F32), "Ts0": ("sbuf", [128, X], BF),
    "L0": ("sbuf", [128, X], BF), "L1": ("sbuf", [128, X], F32), "L2": ("sbuf", [128, X], F32),
    "V": ("sbuf", [128, W], BF), "Vg": ("sbuf", [128, W], BF), "Rw": ("sbuf", [128, W], BF),
    "mS": ("sbuf", [128, 256], F32), "r1": ("sbuf", [128, 3584], BF), "r2": ("sbuf", [128, 3584], BF),
    "Yo": ("sbuf", [128, 2048], F32),
    "Q0": ("sbuf", [128, 256], U16), "Q1": ("sbuf", [128, 256], U16), "Q2": ("sbuf", [128, 256], U16),
    "Qs": ("sbuf", [128, 288], U16), "hy": ("sbuf", [128, 256], F32), "kc": ("sbuf", [128, 160], BF),
    "Qf": ("sbuf", [128, 256], F32), "HL": ("sbuf", [128, 256], BF),
    "it": ("sbuf", [128, 768], I32), "it16": ("sbuf", [128, 768], U16),
    "E": ("sbuf", [128, 768], F32), "En": ("sbuf", [128, 768], F32), "Z2": ("sbuf", [128, 160], BF),
    "Xc": ("sbuf", [128, 256], F32), "Xn": ("sbuf", [128, 256], F32),
    "Wf": ("sbuf", [128, 256], F32), "Wb": ("sbuf", [128, 256], F32),
    "Et": ("sbuf", [128, 256], F32), "Lf": ("sbuf", [128, 256], F32), "Lb": ("sbuf", [128, 256], F32),
    "Lk": ("sbuf", [128, 256], F32), "Rk": ("sbuf", [128, 256], F32), "c2": ("sbuf", [128, 256], F32),
    "Bs": ("sbuf", [128, 2, 128], F32), "IK": ("sbuf", [128, 128], F32),
    "ch": ("sbuf", [128, 256], I32),
    "en": ("sbuf", [128, 256], I32), "su": ("sbuf", [128, 256], F32), "hd": ("sbuf", [128, 256], F32),
    "s16": ("sbuf", [128, 256], U16), "s16a": ("sbuf", [128, 160], U16),
    "rs": ("sbuf", [128, 256], I32), "hrow": ("sbuf", [128, 32], I32), "hb": ("sbuf", [128, 32], I32),
    "hm": ("sbuf", [128, 24], F32), "nh": ("sbuf", [128, 4], F32),
    "i1": ("sbuf", [128, 160], I32), "i2": ("sbuf", [128, 160], I32), "i3": ("sbuf", [128, 160], I32),
    "i4": ("sbuf", [128, 8], I32),
    "pc": ("sbuf", [128, 4], I32), "pm": ("sbuf", [128, 8], I32), "pf": ("sbuf", [128, 8], F32),
    "kb": ("sbuf", [128, 32], BF), "mk": ("sbuf", [128, 256], F32),
    "Iw": ("sbuf", [128, 160], F32), "In": ("sbuf", [128, 160], F32), "Ib": ("sbuf", [128, 128], BF),
    "Inb": ("sbuf", [128, 128], BF), "Z": ("sbuf", [128, 160], BF),
    "Sw": ("sbuf", [128, 2, 128], F32), "Sb": ("sbuf", [128, 2, 128], BF), "Pm": ("sbuf", [128, 8], F32),
    "pv": ("psum", [128, 2048], F32), "pa": ("psum", [128, 512], F32), "pb": ("psum", [128, 512], F32),
    "pk": ("psum", [128, 512], F32), "pt": ("psum", [128, 512], F32),
}
NDMA = 48
SEMAPHORES = ["v", "a", "t", "p", "sent"] + ["d%d" % i for i in range(NDMA)] + ["s%d" % i for i in range(18)] + \
    ["r%d" % i for i in range(18)] + ["h%d" % i for i in range(6)]
ROWED = ("spa", "spb", "reca", "recb", "it", "rs", "hrow", "y")
BIG = float(2 ** 26)
K = float(2 ** 27)
ROUND = 1.5 * 2 ** 35
SPAN = {}
CELLS = {}
P0 = ("Rv0-32 La1 Ta0 Hv Q-0-32 Ta1 Rv64-96 Tv2 Ta3 Ra160-256 Ra96-160 Rv32-64 La2 Q-96-160 Q-32-96 Lv0 Tv4 La4 La3 "
      "M-3072-3584 M-2560-3072 Q-160-256 M-1536-2048 M-2048-2560 X M-3584-4096 Dz2047-2558 M-0-512 Da3840-4096 Da3069-3580 "
      "Wa3069-3580 M-512-960 Da1537-2047 Wa3840-4096 Dz2558-3069 Dp3580-3840 Wz2558-3069 M-960-1536 Dz1280-1537 Wz2047-2558 "
      "Wz1280-1537 S Da1-511 Da1022-1280 Wa1-511 Wp3580-3840 Da511-1022 Wa1022-1280 Wa1537-2047 Wa511-1022")
P1 = ("Ta0 Rv0-64 Ta1 Hv Tv2 Ta3 Ra160-256 La1 Ra96-160 La2 Rv64-96 Q-32-96 Lv0 Q-0-32 Tv4 Q-160-256 Q-96-160 M-2048-2560 "
      "La3 La4 M-3584-4096 X M-3072-3584 M-2560-3072 M-1536-2048 M-0-512 M-512-960 Da3840-4096 Da1537-2047 M-960-1248 "
      "Da3069-3580 Wa3840-4096 M-1248-1536 Dz2047-2558 De3580-3840 Dw1-511 Wa3069-3580 Wa1537-2047 Wz2047-2558 Dp2558-3069 "
      "Da959-1247 Wa959-1247 Da1247-1537 Da511-959 S Wa1247-1537 We3580-3840 Wa511-959 Ww1-511 Wp2558-3069")
P2 = ("Ta0 Tv1 La4 Rv160-256 Ta2 Ta3 Ha Q-160-256 Rv64-160 Ra0-64 La1 Ta4 La3 Q-0-64 M-2048-2560 Q-96-160 M-3584-4096 X "
      "M-0-512 M-3072-3584 Uv1024-1536 Q-64-96 M-960-1280 Yv1024-1280 La0 Uv1536-2048 La2 M-2560-3072 Ua0-512 M-512-960 "
      "M-1280-1536 Uv512-1024 M-1536-2048 Yv512-1024 Yv1536-2048 Yv1280-1536 Ya0-512")
OPT = {"greedy": True, "slack": {"v": 0.1, "a": 0.1, "t": 0.1}, "fit": 0.0, "relay": (1, 2),
       "parts": [[(160, 256), (0, 160)]] * 3, "ilv": [[(0,), (1,)]] * 3,
       "pe": 0.49e-3, "cy": 0.84e-3, "fix": 0.025, "gat": 1.35, "dbw": 500e3, "wake": 0.2,
       "rlat": (0.0, 3.3, 0.0, 3.8, 4.6, 4.2), "rw": 288, "hop": (0.0, 5.7, 3.6), "m0": "pcpppppqp",
       "sp": [0, 528, 1536, 2816, 4096],
       "c0": [1, 512, 1023, 1534, 2045, 2556, 3067, 3578, 3840, 4096],
       "ve": ["avvaavav", "avavavav", "avavavav"], "plan": [P0, P1, P2],
       "pre": "row 0 1 2 lists 4 cnt 5 6 key 3 hops 7 8 moved split late keys"}


def route(T, topo, rank, t):
    src = T.cores[rank]
    dst = T.cores[(rank + 1) % len(T.cores)]
    eng = topo.engines(src, dst)
    relay = None
    if topo.chip(src) != topo.chip(dst) and t in OPT["relay"]:
        for c in topo.cores_of(src):
            if T.rank_of(c) is None and topo.die(c) != topo.die(src) and topo.may_write(c, dst):
                relay = c
    if relay is not None:
        first = [e for e in topo.engines(src, relay) if e not in eng]
        second = eng
    else:
        first, second = eng[len(eng) // 2:], eng[:len(eng) // 2]
    whole = second if relay is not None or topo.chip(src) == topo.chip(dst) else eng
    w = OPT["rw"]
    return dst, [(X - 2 * w, X - w, relay, first), (0, w, None, second), (X - w, X, relay, first), (w, 2 * w, None, second),
                 (2 * w, X - 2 * w, None, whole)], whole


def bits(engines):
    return sum(1 << e for e in engines)


def relay_program(g, core, T, topo):
    for rank in range(len(T.cores)):
        dst, pieces, _e = route(T, topo, rank, 2)
        if pieces[0][2] != core:
            continue
        rid, pid, _s = topo.addr(dst)
        on = topo.engines(core, dst)
        for t in OPT["relay"]:
            buf = T["L%d" % t]
            for i in (0, 2):
                a, b, _r, eng = pieces[i]
                g.wait_ge(T.sem["h%d" % (2 * t + i // 2)], len(eng))
                g.remote_dma(buf[:, a:b], buf[:, a:b], T.sem["r%d" % (6 * t + i)], T.sem["sent"], pid, rid, bits(on))
        g.wait_ge(T.sem["sent"], 2 * len(OPT["relay"]) * len(on))


def rank_program(g, core, T, topo):
    rank = T.rank_of(core)
    if rank is None:
        relay_program(g, core, T, topo)
        return
    N = len(T.cores)
    Q = {"v": g.vector, "a": g.scalar, "t": g.tensor, "p": g, "s": g.sync}
    ops = []
    shapes = {k: v[1] for k, v in SCRATCH.items()}
    shapes["y"] = [128, 2048]
    last_w = {}
    readers = {}

    def R(name, *idx):
        idx = idx if idx else (slice(None),)
        return (name, idx, T[name][idx if len(idx) > 1 else idx[0]])

    def G(win, off):
        return (win, off, win[2].indirect(off[2]))

    def cells(ref):
        name, idx = ref[0], ref[1]
        key = (name, repr(idx))
        if key not in CELLS:
            m = np.zeros(shapes[name], bool)
            m[idx] = True
            m = m.reshape(8, 16, -1).any(axis=1) if name in ROWED else m.reshape(128, -1).any(axis=0)
            if SCRATCH.get(name, ("", ))[0] == "psum":
                m = m.reshape(-1, 512).any(axis=1)
            CELLS[key] = int.from_bytes(np.packbits(m.ravel()).tobytes(), "big")
        return name, CELLS[key]

    def flat(refs):
        out = []
        for r in refs:
            if isinstance(r, tuple) and len(r) == 3:
                if isinstance(r[0], tuple):
                    out += [r[0], r[1]]
                else:
                    out.append(r)
        return out

    def width(ref):
        if isinstance(ref[0], tuple):
            return 16 * width(ref[1])
        return int(np.prod(ref[2].shape[1:]))

    def price(q, writes, reads):
        full = [r for r in reads if isinstance(r, tuple)]
        if q == "t":
            return max(64, width(writes[0])) * OPT["pe"] * (4 if SCRATCH[full[0][0]][2] == F32 else 1)
        n = width(writes[0])
        if any(isinstance(r[0], tuple) for r in full):
            return 0.055 + n * OPT["gat"] * OPT["cy"]
        if q == "p":
            return 0.15 + n * 2 * OPT["cy"]
        big = [r for r in full if width(r) == n]
        if len(big) == 2 and all(SCRATCH[r[0]][0] == "sbuf" for r in big) and n > 1:
            n *= 2
        elif q == "v" and all(SCRATCH[r[0]][2] in (BF, U16) for r in big + writes):
            n //= 2
        return OPT["fix"] + max(64, n) * OPT["cy"]

    def op(q, fn, writes, reads, sem=None, inc=1, cost=None, lat=0.0, after=()):
        me = len(ops)
        deps = set()
        order = set(after)
        for r in flat(reads):
            if r[0] not in shapes:
                continue
            name, c = cells(r)
            psum = SCRATCH.get(name, ("", ))[0] == "psum"
            deps.update(d for d, cc in last_w.get(name, []) if cc & c)
            if psum:
                deps.update(d for d, cc in readers.get(name, []) if ops[d]["q"] != q and cc & c)
            readers.setdefault(name, []).append((me, c))
        for r in flat(writes):
            name, c = cells(r)
            for d, cc in last_w.get(name, []):
                if cc & c:
                    same = ops[d]["q"] == q and sem is None and ops[d]["sem"] is None
                    (order if same and q == "t" else deps).add(d)
            deps.update(d for d, cc in readers.get(name, []) if cc & c)
            readers[name] = [(d, cc & ~c) for d, cc in readers.get(name, []) if cc & ~c]
            last_w[name] = [(d, cc & ~c) for d, cc in last_w.get(name, []) if cc & ~c] + [(me, c)]
        deps.discard(me)
        if cost is None:
            cost = price(q, writes, reads)
        if q in "spr" and not (writes and writes[0][0] == "y"):
            k = "p" if q == "r" else q
            if k in chain:
                (deps if q == "p" else order).add(chain[k])
            chain[k] = me
        ops.append({"q": q, "fn": fn, "deps": deps, "order": order, "sem": sem, "inc": inc, "cost": cost, "lat": lat})
        return me

    nd = [0]
    chain = {}
    moved_us = [0.0]

    def dma(q, out, in_, load=True):
        s = "d%d" % nd[0]
        nd[0] += 1
        us = int(np.prod(out[2].shape)) * (2 if SCRATCH.get(out[0], (0, 0, F32))[2] == BF else 4) / OPT["dbw"]
        if load:
            moved_us[0] += us
            us = moved_us[0]
        op(q, lambda: Q[q].dma_start(out[2], in_[2]), [out], [in_], sem=s, inc=16, cost=0.06, lat=1.8 + us)

    def ap(x):
        return x[2] if isinstance(x, tuple) else x

    def tt(out, a, b, o):
        op("v", lambda: g.vector.tensor_tensor(out[2], a[2], b[2], o), [out], [a, b])

    def ts(out, a, s1, s2, o0, o1=None):
        if o1 is None:
            op("v", lambda: g.vector.tensor_scalar(out[2], a[2], ap(s1), None, o0), [out], [a, s1])
        else:
            op("v", lambda: g.vector.tensor_scalar(out[2], a[2], ap(s1), ap(s2), o0, o1), [out], [a, s1, s2])

    def cp(out, a):
        op("v", lambda: g.vector.tensor_copy(out[2], a[2]), [out], [a])

    def tr(out, a):
        op("v", lambda: g.vector.transpose(out[2], a[2]), [out], [a])

    def scan(out, d0, d1, init, o0, o1):
        op("v", lambda: g.vector.tensor_tensor_scan(out[2], d0[2], d1[2], init, o0, o1), [out], [d0, d1],
           cost=OPT["fix"] + max(64, width(out)) * OPT["cy"])

    def fill(out, c):
        op("v", lambda: g.vector.memset(out[2], c), [out], [])

    def act(out, a, f=AF.Copy, bias=0.0, scale=1.0):
        if f == AF.Copy:
            op("a", lambda: g.scalar.activation(out[2], a[2], f, scale=ap(scale)), [out], [a, scale])
        else:
            op("a", lambda: g.scalar.activation(out[2], a[2], f, bias=ap(bias), scale=ap(scale)), [out], [a, bias, scale])

    def mm(out, l, r, start, stop):
        op("t", lambda: g.tensor.matmul(out[2], l[2], r[2], start, stop), [out], [l, r])

    def iota(out, pat, base, cm, small=False):
        if small:
            op("p", lambda: g.iota(out[2], pat, base, cm, allow_small_or_imprecise_dtypes=True), [out], [])
        else:
            op("p", lambda: g.iota(out[2], pat, base, cm), [out], [])

    S = slice
    ALL = S(None)
    col = lambda name, k: R(name, ALL, S(k, k + 1))

    def turned(q2, buf, cols, src, scols, k, unit=16):
        k %= 8
        dma(q2[0], R(buf, S(0, 128 - 16 * k), *cols), (src, None, T[src][unit * k:unit * 8, scols]))
        if k:
            dma(q2[1], R(buf, S(128 - 16 * k, 128), *cols), (src, None, T[src][0:unit * k, scols]))

    sp = OPT["sp"]
    turned("sa", "spb", (S(sp[0], sp[1]),), "sp", S(sp[0], sp[1]), rank + 1)
    for i in range(1, len(sp) - 1):
        turned("sa", "spb", (S(sp[i], sp[i + 1]),), "sp", S(sp[i], sp[i + 1]), rank + 1)
    turned("ss", "it", (S(0, 256),), "itg", S(0, 256), rank + 1)
    turned("ss", "rs", (ALL,), "rot", ALL, rank + 1, unit=1)
    turned("ss", "it", (S(256, 768),), "itg", S(256, 768), rank)
    dma("s", R("hrow", S(0, 1), S(0, 3 * (8 - rank))), ("hop", None, T.hop[rank:8, :]))
    dma("s", R("hrow", S(0, 1), S(3 * (8 - rank), 27)), ("hop", None, T.hop[0:rank + 1, :]))
    turned("ss", "spa", (ALL,), "sp", ALL, rank)
    for buf, k in (("reca", rank), ("recb", rank + 1)):
        for a, b, c in ((0, 2048, 2048), (2048, 6144, 0), (6144, 2 * W + 16, 0)):
            turned("ss", buf, (S(a, b),), "rec", S(c, c + b - a), k)

    iota(R("i1"), [[1, 160]], 112, -1)
    iota(R("pc"), [[0, 4]], 0, 1)
    iota(R("spb", ALL, S(W, W + 16)), [[0, 16]], 0, 0, True)
    iota(R("V", ALL, S(0, 1)), [[0, 1]], 1, 0, True)
    iota(R("i4"), [[1, 8]], 0, 0)
    iota(R("mk"), [[16, 256]], -2048, 0, True)
    iota(R("Sx", ALL, S(W, W + 8)), [[0, 8]], 0, 0, True)
    iota(R("Sy", ALL, S(W, W + 8)), [[0, 8]], 0, 0, True)
    op("p", lambda: g.partition_broadcast(T.hb[:, 0:27], T.hrow[0:1, 0:27], 128), [R("hb")], [R("hrow", S(0, 1), S(0, 27))])
    ts(R("i2"), R("i1"), 127, None, ALU.bitwise_and)
    ts(R("Ib"), R("i2", ALL, S(16, 144)), 0.0, None, ALU.is_equal)
    act(R("Inb"), R("Ib"), scale=-1.0)

    def count_consts():
        ts(col("pm", 0), col("pc", 0), 15, None, ALU.bitwise_and)
        cp(col("pf", 0), col("pm", 0))
        ts(R("i3"), R("i1"), col("pf", 0), 112.0, ALU.add, ALU.add)
        ts(R("i3"), R("i3"), 127, None, ALU.bitwise_and)
        ts(R("Z"), R("i3"), 0.0, None, ALU.is_equal)
        act(R("Z2"), R("Z"), scale=2 * BIG)
        fill(R("kb"), 2 * BIG)

    def row_consts():
        ts(R("Iw"), R("i2"), 0.0, None, ALU.is_equal)
        ts(col("pm", 4), col("pc", 0), 1, None, ALU.bitwise_and)
        ts(col("pm", 5), col("pc", 0), 1, 7, ALU.logical_shift_right, ALU.bitwise_and)
        cp(R("pf", ALL, S(4, 6)), R("pm", ALL, S(4, 6)))
        ts(col("pf", 3), col("pf", 4), -1.0, 1.0, ALU.mult, ALU.add)
        ts(R("Pm"), R("i4"), col("pf", 5), None, ALU.is_equal)
        for v in range(2):
            act(R("Sw", ALL, v, ALL), R("Iw", ALL, S(15 + 2 * v, 143 + 2 * v)), scale=col("pf", 3 + v))
            act(R("pt", ALL, S(256 + 128 * v, 384 + 128 * v)), R("Iw", ALL, S(16, 144)), scale=col("pf", 3 + v))
        tt(R("Sb"), R("pt", ALL, S(256, 512)), R("Sw"), ALU.subtract)

    def key_consts():
        act(R("mk"), R("mk"), AF.Identity, bias=col("pf", 0))
        act(R("pk", ALL, S(0, 256)), R("mk"), AF.Identity, bias=2048.0, scale=8191.0)

    def late_consts():
        mm(R("pb", ALL, S(0, 128)), R("Z", ALL, S(17, 145)), R("Ib"), True, True)
        mm(R("pb", ALL, S(128, 256)), R("Z", ALL, S(32, 160)), R("Inb"), True, True)
        act(R("Bs"), R("pb", ALL, S(0, 256)))
        act(R("IK"), R("Iw", ALL, S(16, 144)), scale=-K)
        act(R("c2"), R("mk"), AF.Identity, bias=-4096.0, scale=-16382.0)
        act(R("pk", ALL, S(256, 512)), R("mk"), AF.Identity, bias=-2048.0)
        act(R("In"), R("Iw"), scale=-1.0)
        if "Ha" in " ".join(OPT["plan"]):
            act(R("mS"), R("mk"), AF.Identity, bias=2048.0)
            fill(R("kc"), ROUND)

    def lists(t):
        c = S(256 * t, 256 * t + 256)
        cp(R("it16", ALL, c), R("it", ALL, c))

    def keys(t):
        c = S(256 * t, 256 * t + 256)
        tt(R("Et"), R("it", ALL, c), R("pk", ALL, S(0, 256)), ALU.add)
        tr(R("E", ALL, c), R("Et"))
        act(R("En", ALL, c), R("E", ALL, c), scale=-1.0)

    def hops():
        for t in range(3):
            o = 3 if t == 0 else t
            tt(R("hm", ALL, S(8 * t, 8 * t + 8)), R("hb", ALL, S(o, o + 22, 3)), R("Z", ALL, S(32, 145, 16)), ALU.mult)
        for t in range(3):
            op("v", lambda t=t: g.vector.tensor_reduce(T.nh[:, t:t + 1], T.hm[:, 8 * t:8 * t + 8], AX.X, ALU.add, negate=True),
               [R("nh", ALL, S(t, t + 1))], [R("hm", ALL, S(8 * t, 8 * t + 8))])

    spare = [0, 512, 1024, 1536]
    begun = {}

    def bank():
        return spare.pop(0)

    def PB(p0, a, b):
        if p0 < 2048:
            return R("pv", ALL, S(p0 + a, p0 + b))
        return R(("pa", "pb", "pt")[p0 // 512 - 4], ALL, S(a, b))

    def votes(Sn, a, b, mode, finish=True):
        w = b - a
        pos, neg = (R("Ib"), R("Inb")) if Sn == "spb" else (R("Iw", ALL, S(16, 144)), R("In", ALL, S(16, 144)))
        if a not in begun:
            p0 = begun[a] = bank()
            if mode in "pqwz":
                o = PB(p0, 0, w + 1)
                mm(o, pos, R(Sn, ALL, S(a - 1, b)), True, False)
                mm(o, neg, R(Sn, ALL, S(a, b + 1)), False, True)
            elif mode in "eg":
                o = PB(p0, 0, w + 1)
                if mode == "g":
                    mm(o, pos, R(Sn, ALL, S(a - 1, b)), True, True)
                else:
                    act(o, R(Sn, ALL, S(a - 1, b)))
                tt(o, o, R(Sn, ALL, S(a, b + 1)), ALU.subtract)
            elif mode == "c":
                mm(PB(p0, 0, w), pos, R(Sn, ALL, S(a - 1, b - 1)), True, True)
            else:
                act(PB(p0, 0, w), R(Sn, ALL, S(a - 1, b - 1)))
        if not finish:
            return
        p0 = begun.pop(a)
        low, nxt = PB(p0, 0, w), PB(p0, 1, min(w + 1, 512))
        r1, r2, huge = R("r1", ALL, S(p0, p0 + w)), R("r2", ALL, S(p0, p0 + w)), float(2 ** 36)
        if mode == "w":
            act(R("r2", ALL, S(p0, p0 + w + 1)), PB(p0, 0, w + 1))
            ts(r1, r2, huge, 0.0, ALU.mult, ALU.max)
            mm(low, R("Ib"), R("r2", ALL, S(p0 + 1, p0 + w + 1)), True, False)
        elif mode in "pqzeg":
            act(r1, low, AF.Relu, scale=huge)
        if mode == "p":
            tt(R("V", ALL, S(a, b)), nxt, r1, ALU.subtract)
        elif mode in "qwzeg":
            if mode in "zeg":
                act(r2, nxt, AF.Relu, scale=-huge)
                mm(low, R("Inb"), r2, True, False)
            if mode == "q":
                mm(low, pos, R(Sn, ALL, S(a, b)), True, False)
                mm(low, neg, R(Sn, ALL, S(a + 1, b + 1)), False, False)
            mm(low, R("Inb"), r1, False, True)
            act(R("V", ALL, S(a, b)), low)
        else:
            tt(low, low, R(Sn, ALL, S(a + 1, b + 1)), ALU.max)
            tt(R("V", ALL, S(a, b)), R(Sn, ALL, S(a, b)), low, ALU.subtract)
        spare.append(p0)

    def rows_split(t):
        if t == 0:
            ts(R("Qf"), R("rs"), 2048.0, None, ALU.add)
            act(R("HL"), R("Qf"))
            return
        p0 = bank()
        spare.append(p0)
        o = PB(p0, 0, 256)
        cp(R("Et"), R("Q%d" % (t - 1)))
        ts(R("HL"), R("Q%d" % (t - 1)), ROUND, -ROUND, ALU.add, ALU.add)
        mm(o, R("Iw", ALL, S(16, 144)), R("Et"), True, False)
        mm(o, R("Inb"), R("HL"), False, True)
        act(R("Qf"), o, AF.Identity, bias=4096.0)
        act(R("HL"), o, AF.Identity, bias=4096.0)

    def rows(t):
        p0 = held[0]
        for r in range(16):
            c = S(r, W, 16) if t else S(256 * r, 256 * r + 256)
            act(R("Rw", ALL, c), R("pv", ALL, S(p0 + 256 * (r % 2), p0 + 256 * (r % 2) + 256)), scale=col("Pm", r // 2))
        spare.append(p0)

    held = [0]

    def row_parts():
        p0 = held[0] = bank()
        for v in range(2):
            o = R("pv", ALL, S(p0 + 256 * v, p0 + 256 * v + 256))
            mm(o, R("Sw", ALL, v, ALL), R("Qf"), True, False)
            mm(o, R("Sb", ALL, v, ALL), R("HL"), False, True)

    def moved(t):
        spare[:] = [p0 for p0 in spare if p0 < 2048]
        if t:
            row_parts()
        for j in range(4):
            for B in (2 * j, 2 * j + 1):
                src = G(R("V"), R("it16", ALL, S(256 * t + 32 * B, 256 * t + 32 * B + 32)))
                out = R("Vg", ALL, S(512 * B, 512 * B + 512))
                if OPT["ve"][t][B] == "a":
                    act(out, src, AF.Sign, bias=2.0 ** -40)
                else:
                    ts(out, src, 0.0, -15.0 / 32, ALU.is_ge, ALU.add)
            for r in range(16):
                mm(R("pa", ALL, S(64 * j, 64 * j + 64)), R("Z2", ALL, S(32 - r, 160 - r)),
                   R("Vg", ALL, S(1024 * j + r, 1024 * j + 1024, 16)), r == 0, r == 15)
                if r == 0:
                    for B in (2 * j, 2 * j + 1):
                        if OPT["ve"][t][B] == "a":
                            mm(R("pa", ALL, S(32 * B, 32 * B + 32)), R("Ib"), R("kb"), False, False)

    def back(lo, hi, step=1):
        return S(hi - 1, lo - 1 if lo else None, -step)

    def nearest(t):
        parts = [S(a, b) for a, b in OPT["parts"][t]]
        tmp = {}
        for c in parts:
            p0 = bank()
            tmp[c.start] = R("pv", ALL, S(p0, p0 + c.stop - c.start))
            mm(tmp[c.start], R("IK"), R("c2", ALL, c), True, False)
        mm(col("pb", 255), R("Inb"), col("kb", 0), True, True)
        mm(col("pt", 256), R("Ib"), col("kb", 0), True, True)
        tr(R("Xc"), R("pa", ALL, S(0, 256)))
        e0 = 256 * t
        for keys_, j in (("E", 0), ("En", 15)):
            first = R(keys_, ALL, S(e0 + j, e0 + 256, 16))
            tt(first, R("Xc", ALL, S(j, 256, 16)), first, ALU.min)
        scan(R("Wf"), R("Xc"), R("E", ALL, S(e0, e0 + 256)), -BIG, ALU.max, ALU.min)
        scan(R("Wb", ALL, back(0, 256)), R("Xc", ALL, back(0, 256)), R("En", ALL, back(e0, e0 + 256)), -BIG, ALU.max, ALU.min)
        tr(R("Lf"), R("Wf"))
        mm(R("pb", ALL, S(256, 511)), R("Bs", ALL, 0, ALL), R("Lf", ALL, S(0, 255)), True, True)
        tr(R("Lb"), R("Wb"))
        gaps = [len(ops) - 1]
        mm(R("pt", ALL, S(1, 256)), R("Bs", ALL, 1, ALL), R("Lb", ALL, S(1, 256)), True, True)
        act(R("Xn"), R("Lb"), scale=-1.0)
        scan(R("Lk"), R("pb", ALL, S(255, 511)), R("Lf"), -BIG, ALU.max, ALU.max)
        for c in parts:
            mm(tmp[c.start], R("IK"), R("Lk", ALL, c), False, False)
        scan(R("Rk", ALL, back(0, 256)), R("pt", ALL, back(1, 257)), R("Xn", ALL, back(0, 256)), BIG, ALU.min, ALU.min)
        gaps.append(len(ops) - 1)
        for c in parts:
            mm(tmp[c.start], R("IK"), R("Rk", ALL, c), False, True)
        if t < 2:
            first = len(ops)
            keys(t + 1)
            lists(t + 1)
            for i, d in zip(range(first, len(ops)), (gaps[0], gaps[1], gaps[1], gaps[0])):
                ops[i]["order"].add(d)
        for grp in OPT["ilv"][t]:
            cs = [parts[i] for i in grp]
            for c in cs:
                tt(tmp[c.start], tmp[c.start], R("Lk", ALL, c), ALU.max)
            for c in cs:
                tt(R("ch", ALL, c), tmp[c.start], R("Rk", ALL, c), ALU.min)
            for c in cs:
                ts(R("en", ALL, c), R("ch", ALL, c), 8191, None, ALU.bitwise_and)
            for c in cs:
                tt(R("su", ALL, c), R("pk", ALL, S(256 + c.start, 256 + c.stop)), R("en", ALL, c), ALU.add)
            for c in cs:
                ts(R("s16", ALL, c), R("su", ALL, c), 4095.0, None, ALU.min)
                spare.append(tmp[c.start][1][1].start)

    def send_two(t, i0):
        dst, pieces, _e = route(T, topo, rank, t)
        moves, reads = [], []
        for i in (i0, i0 + 1):
            a, b, relay, eng = pieces[i]
            rid, pid, _s = topo.addr(dst if relay is None else relay)
            in_ = R("Ts0" if t == 0 else "Ts", ALL, S(a, b))
            reads.append(in_)
            moves.append(RemoteDMATransfer(dst_ids=[DstId(rid=rid, pnc=pid)], dma_engine_mask=bits(eng),
                                           remote_sem=T.sem["r%d" % (6 * t + i) if relay is None else "h%d" % (2 * t + i // 2)],
                                           src=in_[2], dst=T["L%d" % t][:, a:b]))
        s = "s%d" % (6 * t + i0)
        return op("r", lambda: g.remote_dma_fused(moves, local_sem=T.sem[s]), [], reads, sem=s,
                  inc=len(pieces[0][3]) + len(pieces[1][3]), cost=0.9, lat=OPT["rlat"][i0 + 1])

    def send(t, i):
        dst, pieces, qeng = route(T, topo, rank, t)
        if i < len(pieces):
            a, b, _r, eng = pieces[i]
            out, in_ = R("L%d" % t, ALL, S(a, b)), R("Ts0" if t == 0 else "Ts", ALL, S(a, b))
        else:
            eng = qeng
            out, in_ = R("Q%d" % t, ALL, S(0, 96)), R("Qs", ALL, S(96 * t, 96 * t + 96))
        rs = T.sem["r%d" % (6 * t + i)]
        rid, pid, _s = topo.addr(dst)
        s = "s%d" % (6 * t + i)
        return op("r", lambda: g.remote_dma(out[2], in_[2], rs, T.sem[s], pid, rid, bits(eng)), [], [in_], sem=s,
                  inc=len(eng), cost=0.9, lat=OPT["rlat"][i])

    def arrive(t, sent):
        _d, inpieces, inq = route(T, topo, (rank - 1) % N, t)
        for i, (a, b, relay, eng) in enumerate(inpieces):
            n = len(eng) if relay is None else len(topo.engines(relay, core))
            op("x", None, [R("L%d" % t, ALL, S(a, b))], [], sem="r%d" % (6 * t + i), inc=n,
               cost=OPT["hop"][t] if i in (0, 2) else 0.0, after=[sent[i]])
        op("x", None, [R("Q%d" % t, ALL, S(0, 96))], [], sem="r%d" % (6 * t + len(inpieces)), inc=len(inq), cost=0.0,
           after=[sent[-1]])

    def gath(q, out, win, off):
        if q == "a":
            act(out, G(win, off))
        else:
            cp(out, G(win, off))

    def rgath(q, k0, k1):
        gath(q, R("Vg", ALL, S(16 * k0, 16 * k1)), R("Rw"), R("s16", ALL, S(k0, k1)))

    def rpick(t, k0, k1, pb, by_scalar):
        o = R(pb, ALL, S(k0, k1))
        z = 0 if t == 0 and k0 < 160 else 16
        mm(o, R("In", ALL, S(z, z + 128)), R("hy", ALL, S(k0, k1)), True, False)
        if by_scalar:
            mm(o, R("Ib"), R("kc", ALL, S(0, k1 - k0)), False, False)
        mm(o, R("Iw", ALL, S(z, z + 128)), R("hd", ALL, S(k0, k1)), False, False)
        for r in range(16):
            mm(o, R("Z", ALL, S(z + 16 - r, z + 144 - r)), R("Vg", ALL, S(16 * k0 + r, 16 * k1, 16)), False, r == 15)

    def qlist(t, k0, k1, pb):
        if k0 < 160:
            cp(R("Q%d" % t, ALL, S(96 + k0, 96 + k1)), R(pb, ALL, S(k0, k1)))
        else:
            cp(R("Qs", ALL, S(96 * t + k0 - 160, 96 * t + k1 - 160)), R(pb, ALL, S(k0, k1)))

    def shift(t):
        old = ("spb", "Sx", "Sy")[t]
        new = ("Sx", "Sy", "Sx")[t]
        lwin = R("spa") if t == 0 else R(old, ALL, S(0, W))
        if t == 0:
            mm(R("pb", ALL, S(0, 160)), R("Iw", ALL, S(0, 128)), R("su", ALL, S(0, 160)), True, True)
            ts(R("s16a"), R("pb", ALL, S(0, 160)), 4095.0, None, ALU.min)
        sent = {}

        def mul(a, b):
            rec = "recb" if (t == 2 and a < X) else "reca"
            other = R("L%d" % t, ALL, S(a, b)) if a < X else R("Tl", ALL, S(a - X, b - X))
            tt(R(new, ALL, S(a, b)), G(R(rec), R("Q%d" % t, ALL, S(a // 16, b // 16))), other, ALU.mult)

        nr = 0
        for step in OPT["plan"][t].split():
            what, q, arg = step[0], step[1:2], [int(z) for z in step[2:].split("-") if z]
            if what == "H" and q == "v":
                ts(R("hd"), R("en"), -4096.0, col("nh", t), ALU.add, ALU.mult)
                ts(R("hy"), R("hd"), ROUND, -ROUND, ALU.add, ALU.add)
            elif what == "H":
                e = R("pa", ALL, S(256, 512))
                mm(e, R("In", ALL, S(16, 144)), R("mS"), True, False)
                mm(e, R("Iw", ALL, S(16, 144)), R("su"), False, True)
                act(R("hy"), e, AF.Identity, bias=ROUND, scale=col("nh", t))
                act(R("hd"), e, scale=col("nh", t))
            elif what == "T":
                i = arg[0]
                a, b = route(T, topo, rank, t)[1][i][:2]
                gath(q, R("Ts0" if t == 0 else "Ts", ALL, S(a, b)), R(old, ALL, S(0, W)),
                     R("s16", ALL, S(160 + a // 16, 160 + b // 16)))
                if i in (1, 3):
                    sent[i - 1] = sent[i] = send_two(t, i - 1)
                if i == 4:
                    sent[i] = send(t, i)
            elif what == "R":
                rgath(q, *arg)
            elif what == "Q":
                k0, k1 = arg
                pb = "pa" if k1 == 256 else "pb" if nr % 2 == 0 else "pt"
                nr += 1
                rpick(t, k0, k1, pb, "Ha" in OPT["plan"][t])
                qlist(t, k0, k1, pb)
                if k1 == 256:
                    sent[5] = send(t, 5)
                if nr == OPT["plan"][t].count("Q"):
                    spare.extend((2048, 2560, 3072))
            elif what == "L":
                k0, k1 = 32 * arg[0], 32 * arg[0] + 32
                gath(q, R("Tl", ALL, S(16 * k0, 16 * k1)), lwin, R("s16a" if t == 0 else "s16", ALL, S(k0, k1)))
            elif what == "X":
                arrive(t, [sent[i] for i in range(6)])
            elif what == "M":
                mul(*arg)
            elif what in "DW":
                votes(new, arg[0], arg[1], q, what == "W")
            elif what == "S":
                rows_split(t + 1)
            elif what == "K":
                keys(t + 1)
            elif what == "U":
                c = S(*arg)
                z = 32 if c.start < X else 16
                mm(R("pv", ALL, c), R("Iw", ALL, S(z, z + 128)), R(new, ALL, S(2048 + c.start, 2048 + c.stop)), True, q == "v")
            else:
                c = S(*arg)
                if q == "a":
                    mm(R("pv", ALL, c), R("Iw", ALL, S(16, 144)), R(new, ALL, c), False, True)
                    act(R("Yo", ALL, c), R("pv", ALL, c))
                else:
                    tt(R("Yo", ALL, c), R("pv", ALL, c), R(new, ALL, c), ALU.add)
                store("sa", c, rank + 1 if c.start < X else rank)

    def store(q2, c, k):
        k %= 8
        dma(q2[0], R("y", S(16 * k, 128), c), R("Yo", S(0, 128 - 16 * k), c), False)
        if k:
            dma(q2[1], R("y", S(0, 16 * k), c), R("Yo", S(128 - 16 * k, 128), c), False)

    cuts = OPT["c0"]
    named = {"cnt": count_consts, "row": row_consts, "key": key_consts, "late": late_consts, "lists": lambda: lists(0),
             "hops": hops, "split": lambda: (rows_split(0), row_parts()), "moved": lambda: moved(0), "keys": lambda: keys(0)}
    for step in OPT["pre"].split():
        if step in named:
            named[step]()
        else:
            votes("spb", cuts[int(step)], cuts[int(step) + 1], OPT["m0"][int(step)])
    for t in range(3):
        if t:
            moved(t)
        nearest(t)
        rows(t)
        shift(t)

    n = len(ops)
    succ = [[] for _ in range(n)]
    pred = [[] for _ in range(n)]
    for i, o in enumerate(ops):
        for d in o["deps"] | o["order"]:
            gap = ops[d]["lat"] + OPT["wake"] if d in o["deps"] or o["q"] == "x" else 0.0
            succ[d].append((i, gap))
            pred[i].append((d, gap))
    lanes = ["p" if o["q"] == "r" else o["q"] for o in ops]
    lane = lambda i: lanes[i]
    cost = [o["cost"] for o in ops]

    def lay(order, prv, ready):
        busy, start = {}, [0.0] * n
        for i in order:
            t = max([ready[i]] + [start[d] + cost[d] + gap for d, gap in prv[i]])
            if lanes[i] != "x":
                row = busy.setdefault(lanes[i], [])
                k = len(row)
                while k and row[k - 1][0] > t:
                    k -= 1
                if k and row[k - 1][1] > t:
                    t = row[k - 1][1]
                while k < len(row) and row[k][0] < t + cost[i] + OPT["fit"]:
                    t = max(t, row[k][1])
                    k += 1
                row.insert(k, (t, t + cost[i]))
            start[i] = t
        return start

    def greedy():
        left = [len(p) for p in pred]
        ready, start, pools, free, done = [0.0] * n, [0.0] * n, {}, {}, 0
        for i in range(n):
            if not left[i]:
                pools.setdefault(lanes[i], []).append(i)
        while done < n:
            first, q = min((max(min(ready[i] for i in p), free.get(k, 0.0)), k) for k, p in pools.items() if p)
            i = min(j for j in pools[q] if ready[j] <= first + OPT["slack"].get(q, 0.0))
            pools[q].remove(i)
            done += 1
            start[i] = max(ready[i], free.get(q, 0.0))
            if q != "x":
                free[q] = start[i] + cost[i]
            for j, gap in succ[i]:
                ready[j] = max(ready[j], start[i] + cost[i] + gap)
                left[j] -= 1
                if not left[j]:
                    pools.setdefault(lanes[j], []).append(j)
        return start

    start = greedy() if OPT["greedy"] else lay(range(n), pred, [0.0] * n)
    best = (max(start[i] + cost[i] + ops[i]["lat"] for i in range(n)), start)
    seq = sorted(range(n), key=lambda i: (best[1][i], i))
    SPAN[rank] = best[0]
    place = {i: k for k, i in enumerate(seq)}
    need = set()
    for o in ops:
        latest = {}
        for d in o["deps"]:
            k = ops[d]["sem"] or ops[d]["q"]
            if k not in latest or place[d] > place[latest[k]]:
                latest[k] = d
        o["deps"] = set(latest.values())
        need |= o["deps"]
    count = {}
    mark = [None] * n
    for i in seq:
        o = ops[i]
        if o["sem"] is not None:
            mark[i] = (o["sem"], o["inc"])
        elif i in need:
            count[o["q"]] = count.get(o["q"], 0) + 1
            mark[i] = (o["q"], count[o["q"]])
    known = {}
    clock = [None] * n
    for i in seq:
        o = ops[i]
        if o["q"] == "x":
            clock[i] = {}
            continue
        q = lane(i)
        kn = known.setdefault(q, {})
        for d in sorted(o["deps"], key=lambda d: -place[d]):
            s, val = mark[d]
            if kn.get(s, 0) < val:
                Q[q].wait_ge(T.sem[s], val)
                kn[s] = val
                for s2, v2 in clock[d].items():
                    if kn.get(s2, 0) < v2:
                        kn[s2] = v2
        clock[i] = dict(kn)
        ins = o["fn"]()
        if mark[i] is not None and o["q"] != "r":
            ins.then_inc(T.sem[mark[i][0]], o["inc"])
    total = {}
    for m in mark:
        if m is not None:
            total[m[0]] = max(total.get(m[0], 0), m[1])
    for s, val in total.items():
        if not any(kn.get(s, 0) >= val for kn in known.values()):
            g.sync.wait_ge(T.sem[s], val)
